import numpy as np, ml_dtypes
CORES = [10,34,74,98]
N = 4
BF = ml_dtypes.bfloat16
def gentries(a):
    return np.ascontiguousarray(a.reshape(8, 16, -1).transpose(0, 2, 1)).reshape(8, -1)
def gtable(e):
    e = np.asarray(e); return np.ascontiguousarray(e.reshape(8, -1, 16).transpose(0, 2, 1)).reshape(128, -1).astype(np.int32)
L, B, V, W, DAYS, INTERVALS, H = 48, 64, 3072, 8192, 2, 3, 12
def parts(rng):
    x = rng.integers(28, 100, (N, 8, 1, V)) + rng.integers(-20, 21, (N, 8, 16, V))
    z = rng.integers(0, 65536, (N, 8, V))
    e = rng.integers(-75, 46, (8, 1, W)) + rng.integers(-20, 21, (8, 16, W))
    return x, z, e
def pack(x, z, e):
    x = np.minimum(np.maximum(x, 0), 127).reshape(N, 128, V); e = np.minimum(np.maximum(e, -128), 128).reshape(1, 128, W)
    return {"x": x.astype(np.float32).astype(BF), "boat": np.stack([gtable(a) for a in z]), "enc": np.repeat(e, N, axis=0).astype(np.float32).astype(BF)}
def timed(rng, z, g):
    r = rng.integers(0, W); z[:, g] = r + W * rng.integers(0, 65536 // W, (N, V))
    return (138 * r + 811 * np.arange(DAYS * INTERVALS + DAYS)) % W
def setup_inputs(rng):
    return pack(*parts(rng))
def setup_inputs_ties(rng):
    x, z, e = parts(rng)
    x = rng.integers(20, 100, (1, 8, 16, 1)) + rng.integers(0, 2, (N, 8, 1, V))
    n = rng.choice(np.array([0, H - 1, H - 1, H, H, H + 1, 16]), (8, 1, W)); up = np.argsort(rng.random((8, 16, W)), axis=1) < n
    e = rng.choice(np.array([0, 0, 1, 1, 1, 2]), (8, 1, W)) - 1 + up
    return pack(x, z, e)
def setup_inputs_order(rng):
    x, z, e = parts(rng); b = np.arange(B); k = INTERVALS; q = b % (2 * k)
    st = np.stack([127 - 2 * b, 1 + 2 * b, np.where(q < k, 10 * (k - q), 10 * (3 * k - q)), 64 + 0 * b, np.where(b == 0, 120, np.where(b == B - 1, 127, 1 + 2 * b))])
    kind = rng.integers(0, 6, (N, 8, L)); kind[:, :, :6] = np.arange(6); kind[:, :, L - 6:] = rng.permutation(6)
    s = st[np.minimum(kind, 4)].transpose(0, 1, 3, 2).reshape(N, 8, 1, V)
    x = np.where(np.tile(kind == 5, (1, 1, B))[:, :, None, :], x, s)
    e = np.where(rng.random((8, 16, W)) < rng.random((8, 1, W)), 1, rng.integers(-1, 1, (8, 16, W)))
    return pack(x, z, e)
def setup_inputs_alike(rng):
    x, z, e = parts(rng); zz = z.reshape(N, 8, B, L).copy(); inv = pow(37, -1, W)
    for b in range(1, B):
        c = rng.choice(np.array([0, W - 1]), (N, 8, L))
        zz[:, :, b] = (c - 101 * zz[:, :, b - 1]) % W * inv % W + W * rng.integers(0, 65536 // W, (N, 8, L))
    zz[:, :, :, 1::2] = rng.choice(np.array([0, 65535, 65535, 1]), (N, 8, B, len(range(1, L, 2))))
    e[:, :, 0] = rng.integers(-10, 31, (8, 16)); e[:, :, W - 1] = rng.integers(-30, 11, (8, 16))
    g = rng.permutation(8); odd = np.arange(N)[:, None, None] % 2 == 1
    for i, (c, s) in enumerate(((0, 1), (W - 1, -1))):
        a = rng.integers(0, W, L); b = (c - 811 * DAYS * INTERVALS - 101 * a) % W * inv % W
        zz[:, g[i]] = np.where(odd, b, a) + W * rng.integers(0, 65536 // W, (N, B, L))
        e[g[i]][:, c] = s * rng.integers(112, 129, 16); e[g[i]][:, c + s] = -s * rng.integers(112, 129, 16)
    return pack(x, zz.reshape(N, 8, V), e)
def setup_inputs_flat(rng):
    x, z, e = parts(rng); g = rng.permutation(8); k = INTERVALS; last = (DAYS - 1) * k
    e[g[0]] = -128; e[g[1]] = 128
    x[:, g[1]] = np.where(rng.random((N, 1, V)) < 0.5, x[:, g[1]], 127 * rng.integers(0, 2, (N, 1, V)))
    e[g[2]] = 127; x[:, g[2]] = 127 * rng.integers(0, 2, (N, 16, V))
    e[g[3]] = rng.choice(np.array([-127, -126]), (1, W)); x[:, g[3]] = 127 * rng.integers(0, 2, (N, 1, V))
    c = timed(rng, z, g[4]); e[g[4]][:, c[:k - 1]] = -128; e[g[4]][:, c[k - 1]] = 128
    c = timed(rng, z, g[5]); e[g[5]][:, c[last]] = -128; e[g[5]][:, c[last + 1]] = rng.integers(127, 129, 16)
    c = timed(rng, z, g[6]); e[g[6]][:, c[:-1]] = -128; e[g[6]][:, c[[last, last + k - 1]]] = 0
    b = np.arange(B)[:, None]; s = np.where(b == 0, 120, np.where(b == B - 1, 127, 1 + 2 * b))
    x[:, g[6]] = np.where(rng.random((N, 1, 1, L)) < 0.5, s, x[:, g[6]].reshape(N, 16, B, L)).reshape(N, 16, V)
    return pack(x, z, e)
def setup_inputs_spread(rng):
    x = np.floor(127.99 * np.exp2(-6 * rng.random((N, 8, 1, V))) * rng.random((N, 8, 16, V))).astype(np.int64)
    z = np.minimum(np.exp2(16 * rng.random((N, 8, V))).astype(np.int64), 65535) - 1 + rng.integers(0, 2, (N, 8, V))
    e = np.rint(128 * np.exp2(-7 * rng.random((8, 1, W))) * (0.25 + 0.75 * rng.random((8, 16, W)))).astype(np.int64) * (2 * rng.integers(0, 2, (8, 1, W)) - 1)
    return pack(x, z, e)
def check_inputs(d):
    bad = []
    for k, lo, hi in (("x", 0, 127), ("boat", 0, 65535), ("enc", -128, 128)):
        v = np.asarray(d[k]).astype(np.float32)
        if not np.all((v >= lo) & (v <= hi) & (v == np.floor(v))): bad.append("range of " + k)
    v = np.asarray(d["enc"]).astype(np.float32)
    if not np.all(v == v[:1]): bad.append("enc alike on all ranks")
    return bad
def beats(xi, zi, xj, zj, e, t):
    c = (37 * zi + 101 * zj + 811 * t) & (W - 1)
    v = np.take_along_axis(e, c[:, :, None, :], 3)
    return np.add.reduce((xi + v > xj).astype(np.int64), axis=2) >= H
def reference(x, boat, enc):
    X = x.astype(np.float32).reshape(N, 8, 16, V); E = enc.astype(np.float32).reshape(N, 8, 16, W)
    Z = np.stack([gentries(a) for a in boat]).astype(np.int64)
    for day in range(DAYS):
        rowing = np.ones((N, 8, V), bool); place = np.tile(np.arange(V), (N, 8, 1))
        for k in range(INTERVALS):
            row = rowing.reshape(N, 8, B, L); rival = np.full((N, 8, B, L), -1); last = np.full((N, 8, L), -1)
            for b in range(B):
                rival[:, :, b] = np.where(row[:, :, b], last, -1)
                last = np.where(row[:, :, b], b * L + np.arange(L), last)
            rival = rival.reshape(N, 8, V); j = np.maximum(rival, 0)
            w = beats(X, Z, np.take_along_axis(X, j[:, :, None, :], 3), np.take_along_axis(Z, j, 2), E, day * INTERVALS + k) & (rival >= 0)
            w = w.reshape(N, 8, B, L); bump = np.zeros((N, 8, B, L), bool); before = np.zeros((N, 8, L), bool)
            for b in range(B):
                bump[:, :, b] = w[:, :, b] & ~before
                before = np.where(row[:, :, b], bump[:, :, b], before)
            i0, i1, i2 = np.nonzero(bump.reshape(N, 8, V)); jj = j[i0, i1, i2]
            place[i0, i1, i2] = jj; place[i0, i1, jj] = i2
            rowing[i0, i1, i2] = False; rowing[i0, i1, jj] = False
        X = np.take_along_axis(X, place[:, :, None, :], 3); Z = np.take_along_axis(Z, place, 2)
        hx, hz = np.array(X[1:, :, :, :L]), np.array(Z[1:, :, :L]); fx, fz = np.array(X[:-1, :, :, V - L:]), np.array(Z[:-1, :, V - L:])
        w = beats(hx, hz, fx, fz, E[1:], DAYS * INTERVALS + day); wx = w[:, :, None, :]
        X[1:, :, :, :L] = np.where(wx, fx, hx); Z[1:, :, :L] = np.where(w, fz, hz)
        X[:-1, :, :, V - L:] = np.where(wx, hx, fx); Z[:-1, :, V - L:] = np.where(w, hz, fz)
    return {"yx": X.reshape(N, 128, V).astype(BF), "yb": np.stack([gtable(a) for a in Z]).astype(np.float32)}

@@ -1,0 +1,645 @@
+from concourse.bass import DstId, RemoteDMATransfer
+from concourse.mybir import AluOpType, ActivationFunctionType
+
+A = AluOpType
+ACT = ActivationFunctionType
+AND, SHR = A.bitwise_and, A.logical_shift_right
+C = float(2 ** 25)
+HUGE = float(2 ** 60)
+ONE = 131072.0
+UP = 128.0
+CW = 1040
+WRAP = 1632
+NV, NV0, NV1 = (36, 28, 28), (44, 44, 28), (36, 36, 44)
+OUT = (("v", "y", 0, 72), ("s", "y", 72, 132), ("s", "s", 132, 192))
+PARTS = ((0, 1), (2,))
+
+
+def centred(v):
+    v %= 8192
+    return v - 8192 if v >= 4096 else v
+
+
+INV = centred(pow(101, -1, 8192))
+BETA = centred(37 * INV)
+
+F, H, I, U = "float32", "bfloat16", "int32", "uint16"
+SCRATCH = {}
+for _n, _w, _t in (("xn", 3072, H), ("outb", 3072, H), ("ew", 8192 + WRAP, H), ("bt", 192, I), ("xa", 3 * CW, H), ("xb", 3 * CW, H), ("sel", 2048, H),
+                   ("jb0", 128, H), ("jb1", 128, H), ("jb", 128, H), ("one", 128, H), ("idp", 128, H), ("idn", 128, H), ("blk", 128, H), ("blc", 128, H),
+                   ("pi", 1, I), ("pj", 1, I), ("sv", 8, F), ("io48", 64, I), ("iob", 64, I),
+                   ("pos", 192, F), ("zero", 192, F), ("rst", 192, F), ("neg", 192, H), ("rl", 192, U), ("n1", 192, I), ("n2", 192, I), ("n3", 192, I),
+                   ("wf", 192, I), ("ni", 192, I), ("so", 192, I), ("su", 192, U), ("h1", 6, I), ("h2", 6, I), ("h3", 3, I), ("h4", 3, I), ("h5", 3, I),
+                   ("hu", 12, U), ("hw", 6, I),
+                   ("q1", 12, I), ("q2", 12, I), ("mc", 192, F), ("mm", 96, F), ("mcmp", 192, H), ("mw", 192, F), ("fin", 96, H), ("xe", 96, H),
+                   ("wa", 3, F), ("uf", 3, F), ("nd", 12, F), ("nw", 12, F), ("nm", 12, F), ("zz", 12, F), ("dz", 6, F), ("zm", 6, F),
+                   ("pn", 6, F), ("p1", 6, I), ("p2", 6, I), ("p3", 6, I), ("p4", 6, I), ("yn", 192, F),
+                   ("tx0", 108, F), ("tx1", 108, F), ("rx0", 108, F), ("rx1", 108, F), ("xo", 16 * sum(NV), H),
+                   ("s", 192, F), ("xk", 192, F), ("t", 192, F), ("nk", 192, F), ("ys", 192, F), ("ra", 192, F), ("rb", 192, F), ("ma", 192, H), ("mb", 192, H),
+                   ("cs", 192, I), ("ca", 192, I), ("oi", 192, I), ("cu", 192, U), ("of", 192, U)):
+    SCRATCH[_n] = ("sbuf", [128, _w], _t)
+for _c in range(3):
+    for _n in ("dv", "cmp", "xr", "es"):
+        SCRATCH["%s_%d" % (_n, _c)] = ("sbuf", [128, 1008], H)
+for _c in sorted(set(NV + NV0 + NV1)):
+    SCRATCH["kc%d" % _c] = ("sbuf", [128, 64], H)
+PSUM = ("va", "vb", "z0", "z1", "u0", "u1", "u2", "u3")
+for _n in PSUM:
+    SCRATCH[_n] = ("psum", [128, 512], F)
+QSEM = {"v": "qv", "s": "qs", "p": "qp", "g": "qg"}
+SEMAPHORES = ["qv", "qs", "qp", "qg", "db", "dx", "de", "dw", "o1", "o3", "o4", "o5", "rh0", "rf0", "rh1", "rf1", "loc"]
+
+
+def B(name, a, b, step=1):
+    return (name, a, b, step)
+
+
+def IND(w, o):
+    return ("ind", w, o)
+
+
+def entries(v):
+    return entries(v[1]) + entries(v[2]) if v[0] == "ind" else [v[:3]]
+
+
+def own(x, c, j0, j1, shift=0):
+    a = c * CW + 16 * (j0 + 2 + shift)
+    return B(x, a, a + 16 * (j1 - j0))
+
+
+def win(x, c):
+    return B(x, c * CW, (c + 1) * CW)
+
+
+def xo(c, j0=0, j1=None):
+    a = sum(NV[:c])
+    return B("xo", 16 * (a + j0), 16 * (a + (NV[c] if j1 is None else j1)))
+
+
+def Y(a, b, step=1):
+    return B("va", a, b, step)
+
+
+def ACC(a, b, step=1):
+    return B("va", 192 + a, 192 + b, step)
+
+
+def UT(a, b, step=1):
+    return B("vb", a, b, step)
+
+
+def R(k):
+    return "rb" if k % 2 else "ra"
+
+
+def M(k):
+    return "mb" if k % 2 else "ma"
+
+
+def t_(n, c, a, b, step=1):
+    return B("%s_%d" % (n, c), a, b, step)
+
+
+def zat(c):
+    return "z%d" % (c // 2), 64 * (c % 2)
+
+
+def drain(calls, n=99):
+    for _ in zip(range(n), calls):
+        pass
+
+
+def chain(*sequences):
+    for x in sequences:
+        for y in x:
+            yield y
+
+
+EW, EWX = B("ew", 0, 8192), B("ew", 0, 8192 + WRAP)
+IDP, IDN = B("idp", 0, 128), B("idn", 0, 128)
+
+
+def rank_program(g, core, T, topo):
+    rank = T.rank_of(core)
+    if rank is None:
+        return
+    n_ranks = len(T.cores)
+    up, down = rank > 0, rank < n_ranks - 1
+    queue = {"v": g.vector, "s": g.scalar, "p": g.tensor, "g": g, "y": g.sync}
+    count = {}
+    waited = {}
+    log = {}
+
+    def need(q, sem, val):
+        if waited.get((q, sem), 0) < val:
+            waited[(q, sem)] = val
+            queue[q].wait_ge(T.sem[sem], val)
+
+    def ap(v):
+        if v[0] == "ind":
+            return ap(v[1]).indirect(ap(v[2]))
+        name, a, b, step = v
+        if step == -1:
+            return T[name][:, b - 1:(a - 1 if a > 0 else None):-1]
+        return T[name][:, a:b] if step == 1 else T[name][:, a:b:step]
+
+    def sync(q, reads, writes, sem, n):
+        waits, new = {}, []
+        for kind, views in (("r", reads), ("w", writes)):
+            for v in views:
+                for name, a, b in entries(v):
+                    ps = name in PSUM
+                    for k2, a2, b2, q2, s2, v2 in log.get(name, []):
+                        if not ((ps and q2 != q) or (a < b2 and a2 < b and not (kind == "r" and k2 == "r"))):
+                            continue
+                        if q2 == q == "p":
+                            continue
+                        waits[s2] = max(waits.get(s2, 0), v2)
+                    new.append((name, kind, a, b))
+        for s2 in sorted(waits):
+            need(q, s2, waits[s2])
+        count[sem] = count.get(sem, 0) + n
+        for name, kind, a, b in new:
+            old = log.setdefault(name, [])
+            if kind == "w":
+                old[:] = [e for e in old if not (a <= e[1] and e[2] <= b and (name not in PSUM or e[3] == q))]
+            else:
+                old[:] = [e for e in old if not (e[0] == "r" and e[3] == q and a <= e[1] and e[2] <= b)]
+            old.append((kind, a, b, q, sem, count[sem]))
+
+    def op(q, reads, writes, call):
+        sync(q, reads, writes, QSEM[q], 1)
+        call().then_inc(T.sem[QSEM[q]], 1)
+
+    def tt(out, a, b, o):
+        op("v", [a, b], [out], lambda: g.vector.tensor_tensor(ap(out), ap(a), ap(b), o))
+
+    def ts(out, a, s1, o1, s2=None, o2=None):
+        rd = [a] + ([s1] if isinstance(s1, tuple) else [])
+        p1 = ap(s1) if isinstance(s1, tuple) else s1
+        if o2 is None:
+            op("v", rd, [out], lambda: g.vector.tensor_scalar(ap(out), ap(a), p1, None, o1))
+        else:
+            op("v", rd, [out], lambda: g.vector.tensor_scalar(ap(out), ap(a), p1, s2, o1, o2))
+
+    def cp(out, a):
+        op("v", [a], [out], lambda: g.vector.tensor_copy(ap(out), ap(a)))
+
+    def scan(out, d0, d1, init, o0, o1):
+        op("v", [d0, d1], [out], lambda: g.vector.tensor_tensor_scan(ap(out), ap(d0), ap(d1), init, o0, o1))
+
+    def fill(out, val):
+        op("v", [], [out], lambda: g.vector.memset(ap(out), val))
+
+    def act(out, a, func=ACT.Copy, **kw):
+        op("s", [a], [out], lambda: g.scalar.activation(ap(out), ap(a), func, **kw))
+
+    def mm(out, lhs, rhs, start, stop):
+        op("p", [lhs, rhs], [out], lambda: g.tensor.matmul(ap(out), ap(lhs), ap(rhs), start, stop))
+
+    def dma(q, out, a, sem, out_ap=None, in_ap=None):
+        sync(q, [a] if a else [], [out] if out else [], sem, 16)
+        queue[q].dma_start(ap(out) if out else out_ap, ap(a) if a else in_ap).then_inc(T.sem[sem], 16)
+
+    def gi(out, pattern, base, cm, **kw):
+        op("g", [], [out], lambda: g.iota(ap(out), pattern, base, cm, **kw))
+
+    def gsel(out, a, pattern, cmpop, val, base, cm):
+        op("g", [a], [out], lambda: g.affine_select(ap(out), ap(a), pattern, cmpop, val, base, cm))
+
+    dma("y", B("bt", 0, 192), None, "db", in_ap=T.boat[:])
+    dma("s", B("xn", 0, 3072), None, "dx", in_ap=T.x[:])
+    dma("y", EW, None, "de", in_ap=T.enc[:])
+    dma("y", B("ew", 8192, 8192 + WRAP), None, "dw", in_ap=T.enc[:, 0:WRAP])
+
+    gi(B("pi", 0, 1), [[0, 1]], 0, 1)
+    gi(B("io48", 0, 64), [[48, 64]], 0, 0)
+    gi(B("iob", 0, 64), [[1, 64]], 1, 0)
+    gi(B("jb0", 0, 128), [[0, 8], [1, 16]], 0, 0, allow_small_or_imprecise_dtypes=True)
+    fill(B("one", 0, 128), 1.0)
+    gsel(B("jb1", 0, 128), B("jb0", 0, 128), [[-16, 8], [0, 16]], A.is_ge, -1.0, 0, 1)
+    gsel(B("jb", 0, 128), B("jb1", 0, 128), [[16, 8], [0, 16]], A.is_ge, -1.0, 15, -1)
+    gsel(IDP, B("one", 0, 128), [[-1, 128]], A.is_equal, 0.0, 0, 1)
+    ts(B("pj", 0, 1), B("pi", 0, 1), 15, AND)
+    for c in range(3):
+        ts(B("sv", 4 + c, 5 + c), B("pj", 0, 1), float(16 * c), A.add)
+    for c in range(3):
+        ts(B("rl", 64 * c, 64 * c + 64), B("io48", 0, 64), B("sv", 4 + c, 5 + c), A.add)
+        ts(B("sv", c, c + 1), B("pj", 0, 1), float(CW * c), A.add)
+    for n, v in (("zero", 0.0), ("rst", 1.0), ("neg", -1.0)):
+        fill(B(n, 0, 192), v)
+    fill(B("rst", 0, 192, 64), 0.0)
+    for n in ("ra", "rb"):
+        fill(B(n, 0, 192, 128), 0.0)
+    for c in range(3):
+        fill(B("xa", c * CW, c * CW + 16), 512.0)
+        fill(B("xb", c * CW, c * CW + 16), 512.0)
+    for n in sorted(set(NV + NV0 + NV1)):
+        k = "kc%d" % n
+        fill(B(k, 0, 64), -7.0 * C)
+        fill(B(k, 1, 1 + n), -11.5 * C)
+        fill(B(k, 0, 1), -float(2 ** 30))
+    ts(B("blc", 0, 128), B("jb", 0, 128), 0.0, A.is_ge, C, A.mult)
+    for s in range(16):
+        gsel(B("sel", 128 * s, 128 * s + 128), B("blc", 0, 128), [[0, 8], [1, 16]], A.is_equal, 0.0, -s, 0)
+    ts(B("blk", 0, 128), B("jb", 0, 128), 0.0, A.is_ge)
+    fill(B("vb", 448, 449), 0.0)
+    fill(B("tx0", 102, 105), 0.0)
+    fill(B("tx1", 102, 105), 0.0)
+
+    def relay(c):
+        act(own("xa", c, -1, 63), IND(B("xn", 0, 3072), B("rl", 64 * c, 64 * c + 64)), bias=UP)
+
+    def perm(c):
+        act(own("xb", c, -1, 63), IND(win("xa", c), B("su", 64 * c, 64 * c + 64)))
+
+    def place_words():
+        yield tt(Y(0, 192), B("wf", 0, 192), B("pos", 0, 192), A.add)
+        yield cp(B("ra", 1, 192), Y(0, 191))
+
+    def first_list():
+        yield tt(B("cs", 0, 191), UT(1, 192), B("wf", 0, 191), A.add)
+        yield ts(B("ca", 0, 191), B("cs", 0, 191), 8191, AND)
+        yield cp(B("cu", 0, 191), B("ca", 0, 191))
+
+    turn = [0]
+
+    def bank():
+        turn[0] += 1
+        return "u%d" % (turn[0] % 4)
+
+    def first_diff(x, c, nv):
+        scan(t_("dv", c, 0, 16 * nv), own(x, c, 0, nv, -1), own(x, c, 0, nv), 0.0, A.max, A.subtract)
+
+    def race_v(c, nv):
+        tt(t_("cmp", c, 0, 16 * nv), IND(EW, B("cu", 64 * c, 64 * c + nv)), t_("dv", c, 0, 16 * nv), A.is_gt)
+
+    def races_v(x, p, h):
+        cuts = [(c, j, min(j + h, NV[c])) for c in p for j in range(0, NV[c], h)]
+        for c, j0, j1 in cuts:
+            yield tt(t_("dv", c, 16 * j0, 16 * j1), IND(win(x, c), B("of", 64 * c + j0, 64 * c + j1)), xo(c, j0, j1), A.subtract)
+        for c, j0, j1 in cuts:
+            yield tt(t_("cmp", c, 16 * j0, 16 * j1), IND(EWX, B("cu", 64 * c + j0, 64 * c + j1)), t_("dv", c, 16 * j0, 16 * j1), A.is_gt)
+
+    def race_s(x, p, k, nvs=NV):
+        signs = []
+
+        def enc(c, u, j0, j1):
+            act(t_("es", c, 16 * j0, 16 * j1), IND(EWX if k else EW, B("cu", 64 * c + j0, 64 * c + j1)))
+            mm(B(u, 0, 16 * (j1 - j0)), IDP, t_("es", c, 16 * j0, 16 * j1), False, True)
+
+        def sign():
+            for out, a in signs:
+                act(out, a, ACT.Sign, bias=-0.5)
+        for c in p:
+            nv = nvs[c]
+            na = nv + 2 * ((66 - nv) // 4)
+            halves = ((bank(), nv, na), (bank(), na, 63))
+            if k:
+                act(t_("xr", c, 16 * nv, 1008), IND(win(x, c), B("of", 64 * c + nv, 64 * c + 63)))
+            for i, (u, j0, j1) in enumerate(halves):
+                o = B(u, 0, 16 * (j1 - j0))
+                mm(o, IDP, own(x, c, j0, j1), True, False)
+                mm(o, IDN, t_("xr", c, 16 * j0, 16 * j1) if k else own(x, c, j0, j1, -1), False, False)
+                if not k:
+                    enc(c, u, j0, j1)
+                if i == (1 if k else 0):
+                    sign()
+            if k:
+                for u, j0, j1 in halves:
+                    enc(c, u, j0, j1)
+            signs[:] = [(t_("cmp", c, 16 * j0, 16 * j1), B(u, 0, 16 * (j1 - j0))) for u, j0, j1 in halves]
+        sign()
+
+    def counts(c, k, nvs=NV):
+        z, a = zat(c)
+        mm(B(z, a, a + 64), IDP, B("kc%d" % nvs[c], 0, 64), True, False)
+        if k:
+            mm(B(z, a + 1, a + 64), IDP, B(M(k), 64 * c + 1, 64 * c + 64), False, False)
+        for s in range(16):
+            mm(B(z, a + 1, a + 64), B("sel", 128 * s, 128 * s + 128), t_("cmp", c, s, 1008, 16), False, s == 15)
+
+    def post(p, k):
+        last = k == 2
+        a, b = 64 * p[0], 64 * p[-1] + 64
+        n = b - a
+        zn, z = zat(p[0])
+        vt, vtr = B("vb", 192, 192 + n), B("vb", 192, 192 + n, -1)
+        nbx, nbr = B("vb", 449 - n, 449), B("vb", 448 - n, 448, -1)
+        s, t, x, nk, ys = (B(i, a, b) for i in ("s", "t", "xk", "nk", "ys"))
+        yield scan(s, B("neg", a, b), B(zn, z, z + n), -1.0, A.mult, A.min)
+        yield tt(vt, Y(a, b), s, A.min)
+        yield scan(nbr, B(M(k) if k else "zero", a, b, -1), vtr, 0.0, A.min, A.max)
+        yield tt(t, vt, B(R(k), a, b), A.min)
+        yield tt(x, s, nbx, A.max)
+        if k:
+            yield tt(nk, nbx, B(M(k), a, b), A.subtract)
+        else:
+            yield tt(ACC(a, b), nbx, t, A.max)
+        yield tt(ys if last else Y(a, b), Y(a, b), x, A.subtract)
+        if k:
+            yield tt(ACC(a, b), ACC(a, b), t, A.max)
+        if not last:
+            yield scan(B(R(k + 1), a + 1, b), B("rst", a, b - 1), Y(a, b - 1), 0.0, A.mult, A.max)
+        if k:
+            yield tt(ACC(a, b), ACC(a, b), nk, A.max)
+        if last:
+            yield tt(ACC(a, b), ACC(a, b), ys, A.max)
+            return
+        cs, oi, ca = B("cs", a, b - 1), B("oi", a, b - 1), B("ca", a, b - 1)
+        yield tt(cs, UT(a + 1, b), B(R(k + 1), a + 1, b), A.add)
+        yield ts(B(M(k + 1), a, b), Y(a, b), 0.0, A.is_le, HUGE, A.mult)
+        yield ts(oi, cs, 13, SHR, 0x7F0, AND)
+        yield ts(ca, cs, 8191, AND)
+        yield ts(B("of", a, b - 1), oi, B("sv", 0, 1), A.add)
+        yield ts(B("cu", a, b - 1), ca, float(811 * (k + 1)), A.add)
+
+    def later_intervals(x, more=()):
+        pa, pb = PARTS
+        more = iter(more)
+        for k in range(2):
+            for _ in post(pa, k):
+                drain(more, 1)
+            drain(more)
+            race_s(x, pa, k + 1)
+            lists = post(pb, k)
+            for _ in races_v(x, pa, 18):
+                drain(lists, 1)
+            for c in pa:
+                counts(c, k + 1)
+            drain(lists)
+            race_s(x, pb, k + 1)
+            drain(races_v(x, pb, 64))
+            counts(2, k + 1)
+
+    TS, TW, TU = (6, 54), (0, 105), 3
+    RS, RW, RU = (0, 60), (51, 54), 57
+
+    def heads_and_feet(day, x):
+        tx = "tx%d" % day
+        h1, h2 = B("h1", 0, 6), B("h2", 0, 6)
+        cp(B("h1", 0, 3), ACC(0, 192, 64))
+        cp(B("h1", 3, 6), ACC(63, 192, 64))
+        ts(h2, h1, 13, SHR, 0x7F0, AND)
+        ts(B("h3", 0, 3), B("h1", 0, 3), 8191, AND)
+        ts(B("hw", 0, 6), h1, 65535, AND)
+        ts(B("h4", 0, 3), B("h3", 0, 3), -4096.0, A.add, float(BETA), A.mult)
+        for c in range(3):
+            ts(B("hu", c, 6, 3), B("h2", c, 6, 3), B("sv", c, c + 1), A.add)
+        ts(B("h5", 0, 3), B("h4", 0, 3), 8191, AND)
+        for i in range(2):
+            cp(B(tx, TW[i], TW[i] + 3), B("hw", 3 * i, 3 * i + 3))
+        src = IND(B(x, 0, 3 * CW), B("hu", 0, 6))
+        if day:
+            ts(B(tx, 6, 102), src, -UP, A.add)
+        else:
+            cp(B(tx, 6, 102), src)
+        ts(B(tx, TU, TU + 3), B("h5", 0, 3), float(4096 + 811 * (6 + day)), A.add)
+
+    def send(day):
+        tx, rx = "tx%d" % day, "rx%d" % day
+        calls = ([(rank - 1, 0, 54, "rh%d" % day)] if up else []) + ([(rank + 1, 54, 0, "rf%d" % day)] if down else [])
+        sync("g", [B(tx, 0, 108)], [], "loc", 0)
+        trs = []
+        for i, (r, a, b, sem) in enumerate(calls):
+            es = topo.engines(core, T.cores[r])
+            es = es[i * len(es) // len(calls):(i + 1) * len(es) // len(calls)]
+            rid, pid, _ = topo.addr(T.cores[r])
+            trs.append(RemoteDMATransfer(dst_ids=[DstId(rid=rid, pnc=pid)], dma_engine_mask=sum(1 << e for e in es), remote_sem=T.sem[sem],
+                                         src=T[tx][:, a:a + 54], dst=T[rx][:, b:b + 54]))
+            count["loc"] = count.get("loc", 0) + len(es)
+        g.remote_dma_fused(trs, local_sem=T.sem["loc"])
+        for ok, r, a, sem in ((up, rank - 1, 0, "rf%d" % day), (down, rank + 1, 54, "rh%d" % day)):
+            if ok:
+                fan = (1 if r > 0 else 0) + (1 if r < n_ranks - 1 else 0)
+                count[sem] = len(topo.engines(T.cores[r], core)) // fan
+                log.setdefault(rx, []).append(("w", a, a + 54, "remote", sem, count[sem]))
+
+    sides = [i for i, ok in ((0, up), (1, down)) if ok]
+
+    def at(i):
+        return 3 * sides.index(i)
+
+    def meeting(day, late=()):
+        tx, rx = "tx%d" % day, "rx%d" % day
+        n = 3 * len(sides)
+        lb = n if day else 2 * n
+        hi = 16 * lb
+        for i in sides:
+            l = at(i)
+            u = B(rx, RU, RU + 3) if i else B(tx, TU, TU + 3)
+            w = B(tx, TW[1], TW[1] + 3) if i else B(rx, RW[0], RW[0] + 3)
+            tt(B("q1", l, l + 3), u, w, A.add)
+            if not day:
+                tt(B("q1", n + l, n + l + 3), u if i else UT(1, 192, 64), B("wa", 0, 3) if i else w, A.add)
+        if day:
+            cp(B("p1", 0, n), B(rx, RW[sides[0]], RW[sides[0]] + n))
+        for i in sides:
+            l = 16 * at(i)
+            o, r = B(tx, TS[i], TS[i] + 48), B(rx, RS[i], RS[i] + 48)
+            tt(B("mc", l, l + 48), o if i else r, r if i else o, A.subtract)
+            if i == sides[0]:
+                ts(B("q2", 0, lb), B("q1", 0, lb), 8191, AND)
+            if not day:
+                e = B("xe", 48 * i, 48 * i + 48)
+                tt(B("mc", 16 * n + l, 16 * n + l + 48), e if i else r, r if i else e, A.subtract)
+        p1, p2, p3, p4 = (B(k, 0, n) for k in ("p1", "p2", "p3", "p4"))
+        if day:
+            ts(p2, p1, 8191, AND)
+        cp(B("hu", 0, lb), B("q2", 0, lb))
+        if day:
+            ts(p3, p1, 57344, AND)
+            ts(p4, p2, -4096.0, A.add, float(INV), A.mult)
+        tt(B("mcmp", 0, hi), IND(EW, B("hu", 0, lb)), B("mc", 0, hi), A.is_gt)
+        if day:
+            drain(late)
+            ts(p2, p4, 8191, AND)
+            tt(B("pn", 0, n), p2, p3, A.add)
+            for i in sides:
+                tt(B("nd", at(i), at(i) + 3), B("pn", at(i), at(i) + 3), B("yn", 189 * i, 189 * i + 3), A.subtract)
+        u0, u1 = bank(), bank()
+        mm(B(u0, 0, 16 * n), B("blk", 0, 128), B("mcmp", 0, 16 * n), True, True)
+        for s in range(16):
+            mm(B(u1, 0, lb), B("sel", 128 * s, 128 * s + 128), B("mcmp", s, hi, 16), s == 0, s == 15)
+        return u0, u1
+
+    def outcome(day, u0, u1):
+        tx, rx = "tx%d" % day, "rx%d" % day
+        n = 3 * len(sides)
+        if not day:
+            k = sides[0]
+            tt(B("nd", 0, n), B(rx, RW[k], RW[k] + n), B("hw", 3 * k, 3 * k + n), A.subtract)
+            if down:
+                tt(B("nd", 9, 12), B(rx, RU, RU + 3), B("uf", 0, 3), A.subtract)
+        ts(B("mw", 0, 16 * n), B(u0, 0, 16 * n), 11.5, A.is_gt)
+        ts(B("nw", 0, n), B(u1, 0, n), 11.5 * C, A.is_gt)
+        if not day:
+            ts(B("zz", 0, n), B(u1, n, 2 * n), -11.5 * C, A.add)
+        tt(B("mm", 0, 16 * n), B("mw", 0, 16 * n), B("mc", 0, 16 * n), A.mult)
+        if day:
+            for i in sides:
+                l = 16 * at(i)
+                tt(B("fin", 48 * i, 48 * i + 48), B(tx, TS[i], TS[i] + 48), B("mm", l, l + 48), A.subtract if i else A.add)
+            tt(B("nm", 0, n), B("nw", 0, n), B("nd", 0, n), A.mult)
+            for i in sides:
+                y = B("yn", 189 * i, 189 * i + 3)
+                tt(y, y, B("nm", at(i), at(i) + 3), A.add)
+            return
+        tt(B("nm", 0, n), B("nw", 0, n), B("nd", 0, n), A.mult)
+        if down:
+            tt(B("nm", 9, 12), B("nw", at(1), at(1) + 3), B("nd", 9, 12), A.mult)
+        for i in sides:
+            y = Y(63 * i, 192, 64)
+            tt(y, y, B("nm", at(i), at(i) + 3), A.add)
+        if down:
+            tt(UT(63, 192, 64), UT(63, 192, 64), B("nm", 9, 12), A.add)
+        if up:
+            cp(B("ra", 1, 192, 64), Y(0, 192, 64))
+
+        def strengths():
+            for c in range(3):
+                for i in sides:
+                    a, b = TS[i] + 16 * c, 16 * (at(i) + c)
+                    yield tt(own("xb", c, 63 * i - 1, 63 * i), B(tx, a, a + 16), B("mm", b, b + 16), A.subtract if i else A.add)
+
+        def held(p):
+            z, z0 = zat(p[0])
+            cols = [(at(i) + p[0], at(i) + p[-1] + 1, B(z, z0 + 62 * i + 1, z0 + 64 * len(p), 64)) for i in sides]
+            for a, b, v in cols:
+                yield tt(B("dz", a, b), B("zz", a, b), v, A.subtract)
+            for a, b, v in cols:
+                yield tt(B("zm", a, b), B("nw", a, b), B("dz", a, b), A.mult)
+            for a, b, v in cols:
+                yield tt(v, v, B("zm", a, b), A.add)
+        drain(held(PARTS[0]))
+        return chain(strengths(), held(PARTS[1]))
+
+    def decode(a, b):
+        n2, n3, ni = B("n2", a, b), B("n3", a, b), B("ni", a, b)
+        yield ts(n2, ni, 8191, AND)
+        yield ts(n3, n2, -4096.0, A.add, float(BETA), A.mult)
+        yield ts(B("wf", a, b), ni, 65535, AND)
+        yield ts(n2, n3, 8191, AND)
+        yield ts(UT(a, b), n2, float(4096 + 811 * 3), A.add)
+
+    def numbers(p):
+        a, b = 64 * p[0], 64 * p[-1] + 64
+        n1, n2, n3, ni = (B(n, a, b) for n in ("n1", "n2", "n3", "ni"))
+        yield ts(n2, ni, 8191, AND)
+        yield ts(n3, ni, 57344, AND)
+        yield ts(n1, n2, -4096.0, A.add, float(INV), A.mult)
+        yield
+        yield ts(n2, n1, 8191, AND)
+        yield
+        for c in p:
+            yield tt(B("yn", c, 192, 3), B("n2", 64 * c, 64 * c + 64), B("n3", 64 * c, 64 * c + 64), A.add)
+
+    def sources(p):
+        a, b = 64 * p[0], 64 * p[-1] + 64
+        yield cp(B("ni", a, b), ACC(a, b))
+        yield
+        yield ts(B("so", a, b), B("ni", a, b), 13, SHR, 0x7F0, AND)
+        yield
+        for c in p:
+            yield ts(B("su", c, 192, 3), B("so", 64 * c, 64 * c + 64), B("sv", c, c + 1), A.add)
+
+    n1, n2, n3 = B("n1", 0, 192), B("n2", 0, 192), B("n3", 0, 192)
+    ni, wf, ut = B("ni", 0, 192), B("wf", 0, 192), UT(0, 192)
+    for c in range(3):
+        cp(B("n1", 64 * c, 64 * c + 64), B("bt", c, 192, 3))
+    ts(n2, n1, 101.0, A.mult, 4096.0, A.add)
+    ts(n3, n1, 57344, AND)
+    ts(ni, n2, 8191, AND)
+    ts(n2, n1, 37.0, A.mult, 4096.0, A.add)
+    tt(wf, ni, n3, A.add)
+    ts(n3, n2, 8191, AND)
+    cp(ut, n3)
+    drain(first_list())
+    for c in range(3):
+        relay(c)
+        ts(B("pos", 64 * c, 64 * c + 64), B("iob", 0, 64), ONE, A.mult)
+    ts(IDN, IDP, -1.0, A.mult)
+    for c in range(3):
+        first_diff("xa", c, NV0[c])
+    drain(place_words())
+    for c in range(3):
+        race_v(c, NV0[c])
+    for c in range(3):
+        cp(xo(c), own("xa", c, 0, NV[c]))
+    race_s("xa", (0, 1), 0, NV0)
+    counts(0, 0, NV0)
+    counts(1, 0, NV0)
+    race_s("xa", (2,), 0, NV0)
+    counts(2, 0, NV0)
+    later_intervals("xa")
+
+    drain(post(PARTS[0], 2))
+    cp(B("ni", 0, 128), ACC(0, 128))
+    ts(B("so", 0, 128), B("ni", 0, 128), 13, SHR, 0x7F0, AND)
+    ts(B("su", 0, 128), B("so", 0, 128), B("sv", 0, 1), A.add)
+    perm(0)
+    perm(1)
+    words = decode(0, 128)
+    for _ in post(PARTS[1], 2):
+        drain(words, 1)
+    heads_and_feet(0, "xa")
+    send(0)
+    cp(B("ni", 128, 192), ACC(128, 192))
+    ts(B("so", 128, 192), B("ni", 128, 192), 13, SHR, 0x7F0, AND)
+    words = decode(128, 192)
+    drain(words, 1)
+    ts(B("su", 128, 192), B("so", 128, 192), B("sv", 0, 1), A.add)
+    drain(words, 1)
+    perm(2)
+    drain(words)
+
+    ts(B("wa", 0, 3), B("wf", 62, 192, 64), float((811 * (3 - 6)) % 8192), A.add)
+    words = place_words()
+    for _ in first_list():
+        drain(words, 1)
+    ts(B("uf", 0, 3), UT(63, 192, 64), float(811 * (6 - 3)), A.add)
+    for c in range(3):
+        first_diff("xb", c, NV1[c])
+    race_v(0, NV1[0])
+    race_v(1, NV1[1])
+    for c in range(3):
+        act(B("xe", 16 * c, 16 * c + 16), own("xb", c, 0, 1))
+        act(B("xe", 48 + 16 * c, 64 + 16 * c), own("xb", c, 61, 62))
+    race_s("xb", (0, 1), 0, NV1)
+    counts(0, 0, NV1)
+    banks = meeting(0)
+    counts(1, 0, NV1)
+    race_s("xb", (2,), 0, NV1)
+    race_v(2, NV1[2])
+    counts(2, 0, NV1)
+    for c in range(3):
+        act(xo(c), own("xb", c, 0, NV[c]))
+    later_intervals("xb", outcome(0, *banks))
+
+    drain(post(PARTS[0], 2))
+    ahead = chain(sources(PARTS[0]), numbers(PARTS[0]))
+    for _ in post(PARTS[1], 2):
+        drain(ahead, 1)
+    heads_and_feet(1, "xb")
+    send(1)
+    for _ in sources(PARTS[1]):
+        drain(ahead, 1)
+    first, end = (48 if up else 0), (3024 if down else 3072)
+    for e, q, a, b in OUT:
+        dst, src = B("outb", 16 * a, 16 * b), IND(B("xb", 0, 3 * CW), B("su", a, b))
+        if e == "s":
+            act(dst, src, bias=-UP)
+        else:
+            ts(dst, src, -UP, A.add)
+        a, b = max(16 * a, first), min(16 * b, end)
+        dma(q, None, B("outb", a, b), "o1", out_ap=T.yx[:, a:b])
+    drain(ahead)
+    outcome(1, *meeting(1, numbers(PARTS[1])))
+    if up:
+        dma("s", None, B("fin", 0, 48), "o3", out_ap=T.yx[:, 0:48])
+    if down:
+        dma("y", None, B("fin", 48, 96), "o4", out_ap=T.yx[:, 3024:3072])
+    dma("y" if up else "s", None, B("yn", 0, 192), "o5", out_ap=T.yb[:])
+    for sem in sorted(count):
+        if count[sem]:
+            need("g", sem, count[sem])

@@ -3,16 +3,24 @@ from concourse.mybir import AluOpType, ActivationFunctionType
 
 A = AluOpType
 ACT = ActivationFunctionType
-AND, SHR = A.bitwise_and, A.logical_shift_right
+AND = A.bitwise_and
 C = float(2 ** 25)
 HUGE = float(2 ** 60)
 ONE = 131072.0
 UP = 128.0
 CW = 1040
 WRAP = 1632
-NV, NV0, NV1 = (36, 28, 28), (44, 44, 28), (36, 36, 44)
-OUT = (("v", "y", 0, 72), ("s", "y", 72, 132), ("s", "s", 132, 192))
-PARTS = ((0, 1), (2,))
+NV = ((32, 26, 26), (20, 26, 30))
+XO = max(NV[0][1:] + NV[1][1:])
+PIECE = 16
+OUT = (("v", "y", 0, 48), ("s", "s", 96, 144), ("v", "y", 48, 96), ("s", "s", 144, 192))
+PARTS = ((0,), (1,), (2,))
+CYCLE, GATHER, WAKE, DMA0, RATE, WAY = 0.00092, 1.5, 0.12, 1.8, 250e3, 3.8
+ENDS = ((0, 1, 2),)
+FIRST = 1.5
+AHEAD = 0.1
+PASSES = 4
+LEAD = (2.0, 1.0, 0.0)
 
 
 def centred(v):
@@ -22,32 +30,35 @@ def centred(v):
 
 INV = centred(pow(101, -1, 8192))
 BETA = centred(37 * INV)
+MID = 8192 * 600
 
 F, H, I, U = "float32", "bfloat16", "int32", "uint16"
 SCRATCH = {}
 for _n, _w, _t in (("xn", 3072, H), ("outb", 3072, H), ("ew", 8192 + WRAP, H), ("bt", 192, I), ("xa", 3 * CW, H), ("xb", 3 * CW, H), ("sel", 2048, H),
                    ("jb0", 128, H), ("jb1", 128, H), ("jb", 128, H), ("one", 128, H), ("idp", 128, H), ("idn", 128, H), ("blk", 128, H), ("blc", 128, H),
                    ("pi", 1, I), ("pj", 1, I), ("sv", 8, F), ("io48", 64, I), ("iob", 64, I),
-                   ("pos", 192, F), ("zero", 192, F), ("rst", 192, F), ("neg", 192, H), ("rl", 192, U), ("n1", 192, I), ("n2", 192, I), ("n3", 192, I),
-                   ("wf", 192, I), ("ni", 192, I), ("so", 192, I), ("su", 192, U), ("h1", 6, I), ("h2", 6, I), ("h3", 3, I), ("h4", 3, I), ("h5", 3, I),
-                   ("hu", 12, U), ("hw", 6, I),
-                   ("q1", 12, I), ("q2", 12, I), ("mc", 192, F), ("mm", 96, F), ("mcmp", 192, H), ("mw", 192, F), ("fin", 96, H), ("xe", 96, H),
-                   ("wa", 3, F), ("uf", 3, F), ("nd", 12, F), ("nw", 12, F), ("nm", 12, F), ("zz", 12, F), ("dz", 6, F), ("zm", 6, F),
-                   ("pn", 6, F), ("p1", 6, I), ("p2", 6, I), ("p3", 6, I), ("p4", 6, I), ("yn", 192, F),
-                   ("tx0", 108, F), ("tx1", 108, F), ("rx0", 108, F), ("rx1", 108, F), ("xo", 16 * sum(NV), H),
-                   ("s", 192, F), ("xk", 192, F), ("t", 192, F), ("nk", 192, F), ("ys", 192, F), ("ra", 192, F), ("rb", 192, F), ("ma", 192, H), ("mb", 192, H),
+                   ("zero", 192, H), ("rst", 192, H), ("neg", 192, H), ("rl", 192, U), ("n1", 192, I), ("n2", 192, I), ("n3", 192, I),
+                   ("uw", 384, I), ("ni", 192, I), ("so", 192, I), ("su", 192, U), ("hu", 6, U), ("hv", 12, U),
+                   ("q1", 12, I), ("q2", 12, I), ("mc", 192, F), ("mm", 192, F), ("mcmp", 192, H), ("mw", 192, F), ("fin", 96, H),
+                   ("nd", 12, F), ("nw", 12, F), ("nm", 12, F), ("zz", 12, F), ("dz", 12, F), ("zm", 12, F), ("ow", 12, F),
+                   ("pn", 12, F), ("p1", 12, I), ("p2", 12, I), ("p3", 12, I), ("p4", 12, I), ("yn", 192, F), ("xo", 48 * XO, H),
+                   ("s", 192, F), ("vt", 192, F), ("xk", 192, F), ("t", 192, F), ("nk", 192, F), ("ys", 192, F), ("ma", 192, H), ("mb", 192, H),
                    ("cs", 192, I), ("ca", 192, I), ("oi", 192, I), ("cu", 192, U), ("of", 192, U)):
     SCRATCH[_n] = ("sbuf", [128, _w], _t)
 for _c in range(3):
     for _n in ("dv", "cmp", "xr", "es"):
         SCRATCH["%s_%d" % (_n, _c)] = ("sbuf", [128, 1008], H)
-for _c in sorted(set(NV + NV0 + NV1)):
+for _c in range(6):
+    SCRATCH["tx%d" % _c] = SCRATCH["rx%d" % _c] = ("sbuf", [128, 108], F)
+for _c in sorted(set(NV[0] + NV[1])):
     SCRATCH["kc%d" % _c] = ("sbuf", [128, 64], H)
-PSUM = ("va", "vb", "z0", "z1", "u0", "u1", "u2", "u3")
+PSUM = ("va", "vb", "u0", "u1", "u2", "w0", "w1", "w2")
+Z = 320
 for _n in PSUM:
     SCRATCH[_n] = ("psum", [128, 512], F)
 QSEM = {"v": "qv", "s": "qs", "p": "qp", "g": "qg"}
-SEMAPHORES = ["qv", "qs", "qp", "qg", "db", "dx", "de", "dw", "o1", "o3", "o4", "o5", "rh0", "rf0", "rh1", "rf1", "loc"]
+SEMAPHORES = (["qv", "qs", "qp", "qg", "db", "dx", "de", "dw", "x0", "x1", "x2", "loc"] + ["o%d" % _c for _c in range(len(OUT) + 3)]
+              + ["r%s%d" % (_n, _c) for _n in "hf" for _c in range(6)])
 
 
 def B(name, a, b, step=1):
@@ -59,7 +70,17 @@ def IND(w, o):
 
 
 def entries(v):
-    return entries(v[1]) + entries(v[2]) if v[0] == "ind" else [v[:3]]
+    return entries(v[1]) + entries(v[2]) if v[0] == "ind" else [v]
+
+
+def size(v):
+    return 16 * size(v[2]) if v[0] == "ind" else len(range(v[1], v[2], abs(v[3])))
+
+
+def meet(v, w):
+    if v[0] != w[0] or v[1] >= w[2] or w[1] >= v[2]:
+        return False
+    return v[3] != w[3] or (v[1] - w[1]) % v[3] == 0
 
 
 def own(x, c, j0, j1, shift=0):
@@ -71,9 +92,8 @@ def win(x, c):
     return B(x, c * CW, (c + 1) * CW)
 
 
-def xo(c, j0=0, j1=None):
-    a = sum(NV[:c])
-    return B("xo", 16 * (a + j0), 16 * (a + (NV[c] if j1 is None else j1)))
+def xo(c, j0=0, j1=XO):
+    return B("xo", 16 * (c * XO + j0), 16 * (c * XO + j1))
 
 
 def Y(a, b, step=1):
@@ -84,12 +104,19 @@ def ACC(a, b, step=1):
     return B("va", 192 + a, 192 + b, step)
 
 
+POS = B("va", 384, 448)
+
+
+def R(a, b):
+    return B("vb", a, b)
+
+
 def UT(a, b, step=1):
-    return B("vb", a, b, step)
+    return B("uw", a, b, step)
 
 
-def R(k):
-    return "rb" if k % 2 else "ra"
+def WF(a, b, step=1):
+    return B("uw", 192 + a, 192 + b, step)
 
 
 def M(k):
@@ -100,23 +127,80 @@ def t_(n, c, a, b, step=1):
     return B("%s_%d" % (n, c), a, b, step)
 
 
+def span(p):
+    return 64 * p[0], 64 * p[-1] + 64
+
+
 def zat(c):
-    return "z%d" % (c // 2), 64 * (c % 2)
-
-
-def drain(calls, n=99):
-    for _ in zip(range(n), calls):
-        pass
-
-
-def chain(*sequences):
-    for x in sequences:
-        for y in x:
-            yield y
+    return "w%d" % [p[0] for p in PARTS if c in p][0], Z + 64 * c
 
 
 EW, EWX = B("ew", 0, 8192), B("ew", 0, 8192 + WRAP)
 IDP, IDN = B("idp", 0, 128), B("idn", 0, 128)
+
+
+def in_order(calls):
+    seen = {}
+    for i, c in enumerate(calls):
+        c["after"] = set(c["after"])
+        for kind, views in (("r", c["reads"]), ("w", c["writes"])):
+            for v in views:
+                for k2, w, j in seen.get(v[0], []):
+                    bank = v[0] in PSUM and (calls[j]["q"] != c["q"] or c["q"] == "p")
+                    if j != i and (bank or (meet(v, w) and "w" in (kind, k2))):
+                        c["after"].add(j)
+                old = seen.setdefault(v[0], [])
+                if kind == "w" and v[3] == 1 and v[0] not in PSUM:
+                    old[:] = [e for e in old if not (v[1] <= e[1][1] and e[1][2] <= v[2])]
+                old.append((kind, v, i))
+    gap = lambda j, i: 0.0 if calls[j]["q"] == calls[i]["q"] == "p" else WAKE
+    for c in calls:
+        c["way"], c["next"] = c["time"], []
+    for i in reversed(range(len(calls))):
+        for j in calls[i]["after"]:
+            calls[j]["way"] = max(calls[j]["way"], calls[j]["time"] + gap(j, i) + calls[i]["way"])
+            calls[j]["next"].append(i)
+    free, order = {}, []
+    left = [len(c["after"]) for c in calls]
+    ready = {i: 0.0 for i in range(len(calls)) if not left[i]}
+    while ready:
+        start = {i: max(t, free.get(calls[i]["q"], 0.0)) for i, t in ready.items()}
+        first = min(start, key=lambda i: (start[i], i))
+        q = calls[first]["q"]
+        i = max((i for i in start if calls[i]["q"] == q and start[i] <= start[first] + AHEAD), key=lambda i: (calls[i]["way"] + calls[i]["lead"] - start[i], -i))
+        c = calls[i]
+        del ready[i]
+        free[q] = start[i] + c["hold"]
+        c["end"] = start[i] + c["time"]
+        order.append(i)
+        for j in c["next"]:
+            left[j] -= 1
+            if not left[j]:
+                ready[j] = max(calls[k]["end"] + gap(k, j) for k in calls[j]["after"])
+
+    def place(order, behind):
+        t, busy = {}, {}
+        for i in order:
+            a, n, line = max([t[j] + d for j, d in behind[i]] + [0.0]), calls[i]["hold"], busy.setdefault(calls[i]["q"], [])
+            k = len(line)
+            while k and line[k - 1][1] > a:
+                k -= 1
+            while k < len(line) and line[k][0] < a + n - 1e-9:
+                a = max(a, line[k][1])
+                k += 1
+            line.insert(k, (a, a + n))
+            t[i] = a
+        return t
+    forth = [[(j, calls[j]["time"] + gap(j, i)) for j in c["after"]] for i, c in enumerate(calls)]
+    back = [[(j, calls[j]["hold"] + gap(i, j) + c["time"] - c["hold"]) for j in c["next"]] for i, c in enumerate(calls)]
+    best = (max(c["end"] for c in calls), order)
+    for _ in range(PASSES):
+        t = place(order[::-1], back)
+        order = sorted(order, key=lambda i: -t[i] - calls[i]["hold"])
+        t = place(order, forth)
+        order = sorted(order, key=lambda i: t[i])
+        best = min(best, (max(t[i] + calls[i]["time"] for i in order), order))
+    return best[1]
 
 
 def rank_program(g, core, T, topo):
@@ -126,16 +210,11 @@ def rank_program(g, core, T, topo):
     n_ranks = len(T.cores)
     up, down = rank > 0, rank < n_ranks - 1
     queue = {"v": g.vector, "s": g.scalar, "p": g.tensor, "g": g, "y": g.sync}
-    count = {}
-    waited = {}
-    log = {}
-
-    def need(q, sem, val):
-        if waited.get((q, sem), 0) < val:
-            waited[(q, sem)] = val
-            queue[q].wait_ge(T.sem[sem], val)
+    calls, lead = [], [0.0]
 
     def ap(v):
+        if not isinstance(v, tuple):
+            return v
         if v[0] == "ind":
             return ap(v[1]).indirect(ap(v[2]))
         name, a, b, step = v
@@ -143,44 +222,33 @@ def rank_program(g, core, T, topo):
             return T[name][:, b - 1:(a - 1 if a > 0 else None):-1]
         return T[name][:, a:b] if step == 1 else T[name][:, a:b:step]
 
-    def sync(q, reads, writes, sem, n):
-        waits, new = {}, []
-        for kind, views in (("r", reads), ("w", writes)):
-            for v in views:
-                for name, a, b in entries(v):
-                    ps = name in PSUM
-                    for k2, a2, b2, q2, s2, v2 in log.get(name, []):
-                        if not ((ps and q2 != q) or (a < b2 and a2 < b and not (kind == "r" and k2 == "r"))):
-                            continue
-                        if q2 == q == "p":
-                            continue
-                        waits[s2] = max(waits.get(s2, 0), v2)
-                    new.append((name, kind, a, b))
-        for s2 in sorted(waits):
-            need(q, s2, waits[s2])
-        count[sem] = count.get(sem, 0) + n
-        for name, kind, a, b in new:
-            old = log.setdefault(name, [])
-            if kind == "w":
-                old[:] = [e for e in old if not (a <= e[1] and e[2] <= b and (name not in PSUM or e[3] == q))]
-            else:
-                old[:] = [e for e in old if not (e[0] == "r" and e[3] == q and a <= e[1] and e[2] <= b)]
-            old.append((kind, a, b, q, sem, count[sem]))
+    def note(q, reads, writes, call, time, hold=None, sem=None, n=1, after=()):
+        flat = lambda views: [e for v in views if isinstance(v, tuple) for e in entries(v)]
+        calls.append({"q": q, "reads": flat(reads), "writes": flat(writes), "call": call, "time": time, "hold": time if hold is None else hold,
+                      "lead": lead[0], "sem": sem or QSEM[q], "n": n, "after": after})
+        return len(calls) - 1
 
-    def op(q, reads, writes, call):
-        sync(q, reads, writes, QSEM[q], 1)
-        call().then_inc(T.sem[QSEM[q]], 1)
+    def op(q, reads, writes, call, cycles=None):
+        n = size(writes[0])
+        if reads and reads[0][0] == "ind":
+            time = 0.06 + n * GATHER * CYCLE
+        elif q == "p":
+            time = max(64, n) * CYCLE / 2
+        elif q == "g":
+            time = 0.17 + 2 * n * CYCLE
+        else:
+            narrow = q == "v" and all(SCRATCH[v[0]][2] in (H, U) for v in reads[:2] + writes if isinstance(v, tuple))
+            time = max(64, n * (cycles or (0.5 if narrow else 1))) * CYCLE
+        note(q, reads, writes, call, time)
 
     def tt(out, a, b, o):
-        op("v", [a, b], [out], lambda: g.vector.tensor_tensor(ap(out), ap(a), ap(b), o))
+        op("v", [a, b], [out], lambda: g.vector.tensor_tensor(ap(out), ap(a), ap(b), o), 1 if a[0] in PSUM or b[0] in PSUM else 2)
 
     def ts(out, a, s1, o1, s2=None, o2=None):
-        rd = [a] + ([s1] if isinstance(s1, tuple) else [])
-        p1 = ap(s1) if isinstance(s1, tuple) else s1
         if o2 is None:
-            op("v", rd, [out], lambda: g.vector.tensor_scalar(ap(out), ap(a), p1, None, o1))
+            op("v", [a, s1], [out], lambda: g.vector.tensor_scalar(ap(out), ap(a), ap(s1), None, o1))
         else:
-            op("v", rd, [out], lambda: g.vector.tensor_scalar(ap(out), ap(a), p1, s2, o1, o2))
+            op("v", [a, s1, s2], [out], lambda: g.vector.tensor_scalar(ap(out), ap(a), ap(s1), ap(s2), o1, o2))
 
     def cp(out, a):
         op("v", [a], [out], lambda: g.vector.tensor_copy(ap(out), ap(a)))
@@ -197,9 +265,9 @@ def rank_program(g, core, T, topo):
     def mm(out, lhs, rhs, start, stop):
         op("p", [lhs, rhs], [out], lambda: g.tensor.matmul(ap(out), ap(lhs), ap(rhs), start, stop))
 
-    def dma(q, out, a, sem, out_ap=None, in_ap=None):
-        sync(q, [a] if a else [], [out] if out else [], sem, 16)
-        queue[q].dma_start(ap(out) if out else out_ap, ap(a) if a else in_ap).then_inc(T.sem[sem], 16)
+    def dma(q, out, a, sem, before=0):
+        n = 256 * (before + size(out if isinstance(out, tuple) else a))
+        note(q, [a], [out], lambda: queue[q].dma_start(ap(out), ap(a)), DMA0 + n / RATE, 0.05, sem, 16)
 
     def gi(out, pattern, base, cm, **kw):
         op("g", [], [out], lambda: g.iota(ap(out), pattern, base, cm, **kw))
@@ -207,10 +275,11 @@ def rank_program(g, core, T, topo):
     def gsel(out, a, pattern, cmpop, val, base, cm):
         op("g", [a], [out], lambda: g.affine_select(ap(out), ap(a), pattern, cmpop, val, base, cm))
 
-    dma("y", B("bt", 0, 192), None, "db", in_ap=T.boat[:])
-    dma("s", B("xn", 0, 3072), None, "dx", in_ap=T.x[:])
-    dma("y", EW, None, "de", in_ap=T.enc[:])
-    dma("y", B("ew", 8192, 8192 + WRAP), None, "dw", in_ap=T.enc[:, 0:WRAP])
+    dma("y", B("bt", 0, 192), T.boat[:], "db")
+    dma("s", B("xn", 0, 3072), T.x[:], "dx")
+    dma("y", EW, T.enc[:], "de", 3072)
+    dma("y", B("ew", 8192, 8192 + WRAP), T.enc[:, 0:WRAP], "dw", 3072 + 8192)
+    n_first = len(calls)
 
     gi(B("pi", 0, 1), [[0, 1]], 0, 1)
     gi(B("io48", 0, 64), [[48, 64]], 0, 0)
@@ -223,423 +292,327 @@ def rank_program(g, core, T, topo):
     ts(B("pj", 0, 1), B("pi", 0, 1), 15, AND)
     for c in range(3):
         ts(B("sv", 4 + c, 5 + c), B("pj", 0, 1), float(16 * c), A.add)
-    for c in range(3):
         ts(B("rl", 64 * c, 64 * c + 64), B("io48", 0, 64), B("sv", 4 + c, 5 + c), A.add)
         ts(B("sv", c, c + 1), B("pj", 0, 1), float(CW * c), A.add)
-    for n, v in (("zero", 0.0), ("rst", 1.0), ("neg", -1.0)):
+    for n, v in (("zero", 0.0), ("rst", 1.0), ("neg", -1.0), ("t", 0.0)):
         fill(B(n, 0, 192), v)
     fill(B("rst", 0, 192, 64), 0.0)
-    for n in ("ra", "rb"):
-        fill(B(n, 0, 192, 128), 0.0)
+    fill(B("vb", 0, 400), 0.0)
+    ts(POS, B("iob", 0, 64), ONE, A.mult)
     for c in range(3):
         fill(B("xa", c * CW, c * CW + 16), 512.0)
         fill(B("xb", c * CW, c * CW + 16), 512.0)
-    for n in sorted(set(NV + NV0 + NV1)):
+    for n in sorted(set(NV[0] + NV[1])):
         k = "kc%d" % n
-        fill(B(k, 0, 64), -7.0 * C)
-        fill(B(k, 1, 1 + n), -11.5 * C)
         fill(B(k, 0, 1), -float(2 ** 30))
+        fill(B(k, 1, 1 + n), -11.5 * C)
+        fill(B(k, 1 + n, 64), -7.0 * C)
     ts(B("blc", 0, 128), B("jb", 0, 128), 0.0, A.is_ge, C, A.mult)
     for s in range(16):
         gsel(B("sel", 128 * s, 128 * s + 128), B("blc", 0, 128), [[0, 8], [1, 16]], A.is_equal, 0.0, -s, 0)
     ts(B("blk", 0, 128), B("jb", 0, 128), 0.0, A.is_ge)
-    fill(B("vb", 448, 449), 0.0)
-    fill(B("tx0", 102, 105), 0.0)
-    fill(B("tx1", 102, 105), 0.0)
+    ts(IDN, IDP, -1.0, A.mult)
+    for c in range(3):
+        fill(B("tx%d" % c, 34, 35), 0.0)
+    for p in ENDS:
+        fill(B("tx%d" % (3 + p[0]), 34 * len(p), 35 * len(p)), 0.0)
 
-    def relay(c):
-        act(own("xa", c, -1, 63), IND(B("xn", 0, 3072), B("rl", 64 * c, 64 * c + 64)), bias=UP)
+    def columns(p, k):
+        a, b = span(p)
+        tt(B("cs", a, b - 1), UT(a + 1, b), R(a + 1, b) if k else ACC(a, b - 1), A.add)
+        ts(B("ca", a, b - 1), B("cs", a, b - 1), 8191, AND)
+        ts(B("cu", a, b - 1), B("ca", a, b - 1), float(811 * k), A.add)
 
-    def perm(c):
-        act(own("xb", c, -1, 63), IND(win("xa", c), B("su", 64 * c, 64 * c + 64)))
-
-    def place_words():
-        yield tt(Y(0, 192), B("wf", 0, 192), B("pos", 0, 192), A.add)
-        yield cp(B("ra", 1, 192), Y(0, 191))
-
-    def first_list():
-        yield tt(B("cs", 0, 191), UT(1, 192), B("wf", 0, 191), A.add)
-        yield ts(B("ca", 0, 191), B("cs", 0, 191), 8191, AND)
-        yield cp(B("cu", 0, 191), B("ca", 0, 191))
-
-    turn = [0]
-
-    def bank():
-        turn[0] += 1
-        return "u%d" % (turn[0] % 4)
-
-    def first_diff(x, c, nv):
-        scan(t_("dv", c, 0, 16 * nv), own(x, c, 0, nv, -1), own(x, c, 0, nv), 0.0, A.max, A.subtract)
-
-    def race_v(c, nv):
-        tt(t_("cmp", c, 0, 16 * nv), IND(EW, B("cu", 64 * c, 64 * c + nv)), t_("dv", c, 0, 16 * nv), A.is_gt)
-
-    def races_v(x, p, h):
-        cuts = [(c, j, min(j + h, NV[c])) for c in p for j in range(0, NV[c], h)]
-        for c, j0, j1 in cuts:
-            yield tt(t_("dv", c, 16 * j0, 16 * j1), IND(win(x, c), B("of", 64 * c + j0, 64 * c + j1)), xo(c, j0, j1), A.subtract)
-        for c, j0, j1 in cuts:
-            yield tt(t_("cmp", c, 16 * j0, 16 * j1), IND(EWX, B("cu", 64 * c + j0, 64 * c + j1)), t_("dv", c, 16 * j0, 16 * j1), A.is_gt)
-
-    def race_s(x, p, k, nvs=NV):
-        signs = []
-
-        def enc(c, u, j0, j1):
-            act(t_("es", c, 16 * j0, 16 * j1), IND(EWX if k else EW, B("cu", 64 * c + j0, 64 * c + j1)))
-            mm(B(u, 0, 16 * (j1 - j0)), IDP, t_("es", c, 16 * j0, 16 * j1), False, True)
-
-        def sign():
-            for out, a in signs:
-                act(out, a, ACT.Sign, bias=-0.5)
-        for c in p:
-            nv = nvs[c]
-            na = nv + 2 * ((66 - nv) // 4)
-            halves = ((bank(), nv, na), (bank(), na, 63))
+    def races(day, c, k):
+        x, nv, ew = "xb" if day else "xa", NV[day][k], EWX if k else EW
+        lead[0] = LEAD[c]
+        if not k:
+            scan(t_("dv", c, 0, 16 * nv), own(x, c, 0, nv, -1), own(x, c, 0, nv), 0.0, A.max, A.subtract)
+        for j0 in range(0, nv, PIECE):
+            j1 = min(j0 + PIECE, nv)
+            dv = t_("dv", c, 16 * j0, 16 * j1)
             if k:
-                act(t_("xr", c, 16 * nv, 1008), IND(win(x, c), B("of", 64 * c + nv, 64 * c + 63)))
-            for i, (u, j0, j1) in enumerate(halves):
-                o = B(u, 0, 16 * (j1 - j0))
-                mm(o, IDP, own(x, c, j0, j1), True, False)
-                mm(o, IDN, t_("xr", c, 16 * j0, 16 * j1) if k else own(x, c, j0, j1, -1), False, False)
-                if not k:
-                    enc(c, u, j0, j1)
-                if i == (1 if k else 0):
-                    sign()
+                tt(dv, IND(win(x, c), B("of", 64 * c + j0, 64 * c + j1)), xo(c, j0, j1), A.subtract)
+            tt(t_("cmp", c, 16 * j0, 16 * j1), IND(ew, B("cu", 64 * c + j0, 64 * c + j1)), dv, A.is_gt)
+        na = max(nv + 2 * ((66 - nv) // 4), 44)
+        for u, j0, j1 in (("u", nv, na), ("w", na, 63)):
+            o = B("%s%d" % (u, c), 0, 16 * (j1 - j0))
+            xr, es = t_("xr", c, 16 * j0, 16 * j1), t_("es", c, 16 * j0, 16 * j1)
+            mm(o, IDP, own(x, c, j0, j1), True, False)
             if k:
-                for u, j0, j1 in halves:
-                    enc(c, u, j0, j1)
-            signs[:] = [(t_("cmp", c, 16 * j0, 16 * j1), B(u, 0, 16 * (j1 - j0))) for u, j0, j1 in halves]
-        sign()
-
-    def counts(c, k, nvs=NV):
+                act(xr, IND(win(x, c), B("of", 64 * c + j0, 64 * c + j1)))
+            mm(o, IDN, xr if k else own(x, c, j0, j1, -1), False, False)
+            act(es, IND(ew, B("cu", 64 * c + j0, 64 * c + j1)))
+            mm(o, IDP, es, False, True)
+            act(t_("cmp", c, 16 * j0, 16 * j1), o, ACT.Sign, bias=-0.5)
         z, a = zat(c)
-        mm(B(z, a, a + 64), IDP, B("kc%d" % nvs[c], 0, 64), True, False)
+        mm(B(z, a, a + 64), IDP, B("kc%d" % nv, 0, 64), True, False)
         if k:
             mm(B(z, a + 1, a + 64), IDP, B(M(k), 64 * c + 1, 64 * c + 64), False, False)
         for s in range(16):
             mm(B(z, a + 1, a + 64), B("sel", 128 * s, 128 * s + 128), t_("cmp", c, s, 1008, 16), False, s == 15)
 
     def post(p, k):
-        last = k == 2
-        a, b = 64 * p[0], 64 * p[-1] + 64
-        n = b - a
-        zn, z = zat(p[0])
-        vt, vtr = B("vb", 192, 192 + n), B("vb", 192, 192 + n, -1)
-        nbx, nbr = B("vb", 449 - n, 449), B("vb", 448 - n, 448, -1)
-        s, t, x, nk, ys = (B(i, a, b) for i in ("s", "t", "xk", "nk", "ys"))
-        yield scan(s, B("neg", a, b), B(zn, z, z + n), -1.0, A.mult, A.min)
-        yield tt(vt, Y(a, b), s, A.min)
-        yield scan(nbr, B(M(k) if k else "zero", a, b, -1), vtr, 0.0, A.min, A.max)
-        yield tt(t, vt, B(R(k), a, b), A.min)
-        yield tt(x, s, nbx, A.max)
+        a, b = span(p)
+        lead[0] = LEAD[p[0]]
+        o = 192 + a + PARTS.index(p)
+        nbr, nbx = B("vb", o, o + b - a, -1), B("vb", o + 1, o + 1 + b - a)
+        s, vt, t, x, nk, ys = (B(i, a, b) for i in ("s", "vt", "t", "xk", "nk", "ys"))
+        scan(s, B("neg", a, b), B(zat(p[0])[0], Z + a, Z + b), -1.0, A.mult, A.min)
+        tt(vt, Y(a, b), s, A.min)
+        scan(nbr, B(M(k) if k else "zero", a, b, -1), B("vt", a, b, -1), 0.0, A.min, A.max)
         if k:
-            yield tt(nk, nbx, B(M(k), a, b), A.subtract)
+            tt(t, R(a, b), vt, A.min)
+            tt(ACC(a, b), ACC(a, b), t, A.max)
+            tt(nk, nbx, B(M(k), a, b), A.subtract)
         else:
-            yield tt(ACC(a, b), nbx, t, A.max)
-        yield tt(ys if last else Y(a, b), Y(a, b), x, A.subtract)
-        if k:
-            yield tt(ACC(a, b), ACC(a, b), t, A.max)
-        if not last:
-            yield scan(B(R(k + 1), a + 1, b), B("rst", a, b - 1), Y(a, b - 1), 0.0, A.mult, A.max)
-        if k:
-            yield tt(ACC(a, b), ACC(a, b), nk, A.max)
-        if last:
-            yield tt(ACC(a, b), ACC(a, b), ys, A.max)
+            tt(B("t", a + 1, b), Y(a, b - 1), B("vt", a + 1, b), A.min)
+            tt(ACC(a, b), nbx, t, A.max)
+        if k == 2:
+            ts(x, s, 0.0, A.max)
+            tt(ys, Y(a, b), x, A.subtract)
+            tt(ACC(a, b), ACC(a, b), ys, A.max)
+            tt(ACC(a, b), ACC(a, b), nk, A.max)
+            cp(B("ni", a, b), ACC(a, b))
+            ts(B("so", a, b), ACC(a, b), 1 / ONE, A.mult, -0.25, A.add)
+            ts(B("n2", a, b), B("ni", a, b), 8191, AND)
             return
-        cs, oi, ca = B("cs", a, b - 1), B("oi", a, b - 1), B("ca", a, b - 1)
-        yield tt(cs, UT(a + 1, b), B(R(k + 1), a + 1, b), A.add)
-        yield ts(B(M(k + 1), a, b), Y(a, b), 0.0, A.is_le, HUGE, A.mult)
-        yield ts(oi, cs, 13, SHR, 0x7F0, AND)
-        yield ts(ca, cs, 8191, AND)
-        yield ts(B("of", a, b - 1), oi, B("sv", 0, 1), A.add)
-        yield ts(B("cu", a, b - 1), ca, float(811 * (k + 1)), A.add)
+        tt(x, nbx, s, A.max)
+        tt(Y(a, b), Y(a, b), x, A.subtract)
+        scan(R(a + 1, b), B("rst", a, b - 1), Y(a, b - 1), 0.0, A.mult, A.max)
+        ts(B(M(k + 1), a, b), Y(a, b), 0.0, A.is_le, HUGE, A.mult)
+        ts(B("oi", a, b - 1), R(a + 1, b), 1 / ONE, A.mult, -0.25, A.add)
+        ts(B("of", a, b - 1), B("oi", a, b - 1), 16.0, A.mult, B("sv", 0, 1), A.add)
+        columns(p, k + 1)
+        if k:
+            tt(ACC(a, b), ACC(a, b), nk, A.max)
 
-    def later_intervals(x, more=()):
-        pa, pb = PARTS
-        more = iter(more)
+    def later_intervals(day):
         for k in range(2):
-            for _ in post(pa, k):
-                drain(more, 1)
-            drain(more)
-            race_s(x, pa, k + 1)
-            lists = post(pb, k)
-            for _ in races_v(x, pa, 18):
-                drain(lists, 1)
-            for c in pa:
-                counts(c, k + 1)
-            drain(lists)
-            race_s(x, pb, k + 1)
-            drain(races_v(x, pb, 64))
-            counts(2, k + 1)
+            for p in PARTS:
+                post(p, k)
+            for c in range(3):
+                races(day, c, k + 1)
 
-    TS, TW, TU = (6, 54), (0, 105), 3
-    RS, RW, RU = (0, 60), (51, 54), 57
-
-    def heads_and_feet(day, x):
-        tx = "tx%d" % day
-        h1, h2 = B("h1", 0, 6), B("h2", 0, 6)
-        cp(B("h1", 0, 3), ACC(0, 192, 64))
-        cp(B("h1", 3, 6), ACC(63, 192, 64))
-        ts(h2, h1, 13, SHR, 0x7F0, AND)
-        ts(B("h3", 0, 3), B("h1", 0, 3), 8191, AND)
-        ts(B("hw", 0, 6), h1, 65535, AND)
-        ts(B("h4", 0, 3), B("h3", 0, 3), -4096.0, A.add, float(BETA), A.mult)
-        for c in range(3):
-            ts(B("hu", c, 6, 3), B("h2", c, 6, 3), B("sv", c, c + 1), A.add)
-        ts(B("h5", 0, 3), B("h4", 0, 3), 8191, AND)
-        for i in range(2):
-            cp(B(tx, TW[i], TW[i] + 3), B("hw", 3 * i, 3 * i + 3))
-        src = IND(B(x, 0, 3 * CW), B("hu", 0, 6))
-        if day:
-            ts(B(tx, 6, 102), src, -UP, A.add)
-        else:
-            cp(B(tx, 6, 102), src)
-        ts(B(tx, TU, TU + 3), B("h5", 0, 3), float(4096 + 811 * (6 + day)), A.add)
-
-    def send(day):
-        tx, rx = "tx%d" % day, "rx%d" % day
-        calls = ([(rank - 1, 0, 54, "rh%d" % day)] if up else []) + ([(rank + 1, 54, 0, "rf%d" % day)] if down else [])
-        sync("g", [B(tx, 0, 108)], [], "loc", 0)
-        trs = []
-        for i, (r, a, b, sem) in enumerate(calls):
-            es = topo.engines(core, T.cores[r])
-            es = es[i * len(es) // len(calls):(i + 1) * len(es) // len(calls)]
-            rid, pid, _ = topo.addr(T.cores[r])
-            trs.append(RemoteDMATransfer(dst_ids=[DstId(rid=rid, pnc=pid)], dma_engine_mask=sum(1 << e for e in es), remote_sem=T.sem[sem],
-                                         src=T[tx][:, a:a + 54], dst=T[rx][:, b:b + 54]))
-            count["loc"] = count.get("loc", 0) + len(es)
-        g.remote_dma_fused(trs, local_sem=T.sem["loc"])
-        for ok, r, a, sem in ((up, rank - 1, 0, "rf%d" % day), (down, rank + 1, 54, "rh%d" % day)):
-            if ok:
-                fan = (1 if r > 0 else 0) + (1 if r < n_ranks - 1 else 0)
-                count[sem] = len(topo.engines(T.cores[r], core)) // fan
-                log.setdefault(rx, []).append(("w", a, a + 54, "remote", sem, count[sem]))
+    def place_words(p):
+        for c in p:
+            tt(Y(64 * c, 64 * c + 64), POS, WF(64 * c, 64 * c + 64), A.add)
 
     sides = [i for i, ok in ((0, up), (1, down)) if ok]
 
-    def at(i):
-        return 3 * sides.index(i)
+    def send(day, p):
+        m, n, (a, b) = 3 * day + p[0], len(p), span(p)
+        tx, rx, hu, w = "tx%d" % m, "rx%d" % m, B("hu", 2 * p[0], 2 * p[0] + 2 * n), 18 * n
+        for j, c in enumerate(p):
+            ts(B("hu", 2 * p[0] + j, 2 * p[0] + 2 * n, n), B("so", 64 * c, 64 * c + 64, 63), 16.0, A.mult, B("sv", j, j + 1), A.add)
+        src = IND(B("xb" if day else "xa", p[0] * CW, (p[-1] + 1) * CW), hu)
+        if day:
+            ts(B(tx, 2 * n, 34 * n), src, -UP, A.add)
+        else:
+            cp(B(tx, 2 * n, 34 * n), src)
+        if n == 1:
+            cp(B(tx, 0, 36, 35), (ACC if day else WF)(a, b, 63))
+        else:
+            for i in range(2):
+                cp(B(tx, 35 * n * i, 35 * n * i + n), ACC(a + 63 * i, b, 64))
+        ts(B(tx, n, 2 * n), B("n2", a, b, 64), float(BETA), A.mult, float(811 * (7 if day else 3) - MID), A.add)
+        ways = ([(rank - 1, 0, w, "rh%d" % m)] if up else []) + ([(rank + 1, w, 0, "rf%d" % m)] if down else [])
+        trs, n = [], 0
+        for i, (r, a, b, sem) in enumerate(ways):
+            es = topo.engines(core, T.cores[r])
+            es = es[i * len(es) // len(ways):(i + 1) * len(es) // len(ways)]
+            rid, pid, _ = topo.addr(T.cores[r])
+            trs.append(RemoteDMATransfer(dst_ids=[DstId(rid=rid, pnc=pid)], dma_engine_mask=sum(1 << e for e in es), remote_sem=T.sem[sem],
+                                         src=T[tx][:, a:a + w], dst=T[rx][:, b:b + w]))
+            n += len(es)
+        sent = note("g", [B(tx, 0, 2 * w)], [], lambda: g.remote_dma_fused(trs, local_sem=T.sem["loc"]), 0.3, None, "loc", n)
+        for ok, r, a, sem in ((up, rank - 1, 0, "rf%d" % m), (down, rank + 1, w, "rh%d" % m)):
+            if ok:
+                fan = (1 if r > 0 else 0) + (1 if r < n_ranks - 1 else 0)
+                note(sem, [], [B(rx, a, a + w)], None, WAY + (0 if m else FIRST), 0.0, sem, len(topo.engines(T.cores[r], core)) // fan, [sent])
 
-    def meeting(day, late=()):
-        tx, rx = "tx%d" % day, "rx%d" % day
-        n = 3 * len(sides)
-        lb = n if day else 2 * n
-        hi = 16 * lb
-        for i in sides:
-            l = at(i)
-            u = B(rx, RU, RU + 3) if i else B(tx, TU, TU + 3)
-            w = B(tx, TW[1], TW[1] + 3) if i else B(rx, RW[0], RW[0] + 3)
-            tt(B("q1", l, l + 3), u, w, A.add)
+    def meetings(day, c):
+        lead[0] = LEAD[c]
+        tx, rx, u, m = "tx%d" % (3 * day + c), "rx%d" % (3 * day + c), "u%d" % c, len(sides)
+        lb = m if day else 2 * m
+        both = lambda name, a, step: B(name, a + step * sides[0], a + step * sides[-1] + 1, step)
+        at = lambda name, a=0, b=m, w=1: B(name, w * (4 * c + a), w * (4 * c + b))
+        if day:
+            tt(at("q1"), both(rx, 17, 2), both(tx, 1, 34), A.add)
+        else:
+            ts(at("ow"), both(tx, 1, 34), float(811 * 3), A.add)
+            tt(at("q1"), both(rx, 17, 2), at("ow"), A.add)
+            tt(at("q1", m, lb), both(rx, 17, 2), both("uw", 64 * c + 1, 253), A.add)
+        for l, i in enumerate(sides):
+            o, r = B(tx, 2 + 16 * i, 18 + 16 * i), B(rx, 20 * i, 20 * i + 16)
+            tt(at("mc", l, l + 1, 16), o if i else r, r if i else o, A.subtract)
             if not day:
-                tt(B("q1", n + l, n + l + 3), u if i else UT(1, 192, 64), B("wa", 0, 3) if i else w, A.add)
+                e = own("xb", c, 61 * i, 61 * i + 1)
+                tt(at("mc", m + l, m + l + 1, 16), e if i else r, r if i else e, A.subtract)
+        ts(at("q2", 0, lb), at("q1", 0, lb), 8191, AND)
+        cp(at("hv", 0, lb), at("q2", 0, lb))
+        tt(at("mcmp", 0, lb, 16), IND(EW, at("hv", 0, lb)), at("mc", 0, lb, 16), A.is_gt)
+
+        def rows():
+            mm(B(u, 16, 16 + 16 * m), B("blk", 0, 128), at("mcmp", 0, m, 16), True, True)
+            ts(at("mw", 0, m, 16), B(u, 16, 16 + 16 * m), 11.5, A.is_gt)
+            tt(at("mm", 0, m, 16), at("mw", 0, m, 16), at("mc", 0, m, 16), A.mult)
+            for l, i in enumerate(sides):
+                new = B("fin", 48 * i + 16 * c, 48 * i + 16 * c + 16) if day else own("xb", c, 63 * i - 1, 63 * i)
+                tt(new, B(tx, 2 + 16 * i, 18 + 16 * i), at("mm", l, l + 1, 16), A.subtract if i else A.add)
         if day:
-            cp(B("p1", 0, n), B(rx, RW[sides[0]], RW[sides[0]] + n))
-        for i in sides:
-            l = 16 * at(i)
-            o, r = B(tx, TS[i], TS[i] + 48), B(rx, RS[i], RS[i] + 48)
-            tt(B("mc", l, l + 48), o if i else r, r if i else o, A.subtract)
-            if i == sides[0]:
-                ts(B("q2", 0, lb), B("q1", 0, lb), 8191, AND)
-            if not day:
-                e = B("xe", 48 * i, 48 * i + 48)
-                tt(B("mc", 16 * n + l, 16 * n + l + 48), e if i else r, r if i else e, A.subtract)
-        p1, p2, p3, p4 = (B(k, 0, n) for k in ("p1", "p2", "p3", "p4"))
-        if day:
-            ts(p2, p1, 8191, AND)
-        cp(B("hu", 0, lb), B("q2", 0, lb))
-        if day:
-            ts(p3, p1, 57344, AND)
-            ts(p4, p2, -4096.0, A.add, float(INV), A.mult)
-        tt(B("mcmp", 0, hi), IND(EW, B("hu", 0, lb)), B("mc", 0, hi), A.is_gt)
-        if day:
-            drain(late)
-            ts(p2, p4, 8191, AND)
-            tt(B("pn", 0, n), p2, p3, A.add)
-            for i in sides:
-                tt(B("nd", at(i), at(i) + 3), B("pn", at(i), at(i) + 3), B("yn", 189 * i, 189 * i + 3), A.subtract)
-        u0, u1 = bank(), bank()
-        mm(B(u0, 0, 16 * n), B("blk", 0, 128), B("mcmp", 0, 16 * n), True, True)
+            rows()
+            u = "w%d" % c
         for s in range(16):
-            mm(B(u1, 0, lb), B("sel", 128 * s, 128 * s + 128), B("mcmp", s, hi, 16), s == 0, s == 15)
-        return u0, u1
-
-    def outcome(day, u0, u1):
-        tx, rx = "tx%d" % day, "rx%d" % day
-        n = 3 * len(sides)
-        if not day:
-            k = sides[0]
-            tt(B("nd", 0, n), B(rx, RW[k], RW[k] + n), B("hw", 3 * k, 3 * k + n), A.subtract)
-            if down:
-                tt(B("nd", 9, 12), B(rx, RU, RU + 3), B("uf", 0, 3), A.subtract)
-        ts(B("mw", 0, 16 * n), B(u0, 0, 16 * n), 11.5, A.is_gt)
-        ts(B("nw", 0, n), B(u1, 0, n), 11.5 * C, A.is_gt)
-        if not day:
-            ts(B("zz", 0, n), B(u1, n, 2 * n), -11.5 * C, A.add)
-        tt(B("mm", 0, 16 * n), B("mw", 0, 16 * n), B("mc", 0, 16 * n), A.mult)
+            mm(B(u, 0, lb), B("sel", 128 * s, 128 * s + 128), B("mcmp", 64 * c + s, 64 * c + 16 * lb, 16), s == 0, s == 15)
+        ts(at("nw"), B(u, 0, m), 11.5 * C, A.is_gt)
         if day:
-            for i in sides:
-                l = 16 * at(i)
-                tt(B("fin", 48 * i, 48 * i + 48), B(tx, TS[i], TS[i] + 48), B("mm", l, l + 48), A.subtract if i else A.add)
-            tt(B("nm", 0, n), B("nw", 0, n), B("nd", 0, n), A.mult)
-            for i in sides:
-                y = B("yn", 189 * i, 189 * i + 3)
-                tt(y, y, B("nm", at(i), at(i) + 3), A.add)
+            cp(at("p1"), both(rx, 17, 1))
+            ts(at("p2"), at("p1"), 8191, AND)
+            ts(at("p3"), at("p1"), 57344, AND)
+            ts(at("p4"), at("p2"), -4096.0, A.add, float(INV), A.mult)
+            ts(at("p1"), at("p4"), 8191, AND)
+            tt(at("pn"), at("p1"), at("p3"), A.add)
+            y = both("yn", c, 189)
+            tt(at("nd"), at("pn"), y, A.subtract)
+            tt(at("nm"), at("nw"), at("nd"), A.mult)
+            tt(y, y, at("nm"), A.add)
             return
-        tt(B("nm", 0, n), B("nw", 0, n), B("nd", 0, n), A.mult)
+        z, y = both(zat(c)[0], zat(c)[1] + 1, 62), both("va", 64 * c, 63)
+        ts(at("zz"), z, 11.5 * C, A.add)
+        tt(at("dz"), B(u, m, lb), at("zz"), A.subtract)
+        tt(at("zm"), at("nw"), at("dz"), A.mult)
+        tt(z, z, at("zm"), A.add)
+        tt(at("nd"), both(rx, 17, 1), both(tx, 0, 35), A.subtract)
+        tt(at("nm"), at("nw"), at("nd"), A.mult)
+        tt(y, y, at("nm"), A.add)
         if down:
-            tt(B("nm", 9, 12), B("nw", at(1), at(1) + 3), B("nd", 9, 12), A.mult)
-        for i in sides:
-            y = Y(63 * i, 192, 64)
-            tt(y, y, B("nm", at(i), at(i) + 3), A.add)
-        if down:
-            tt(UT(63, 192, 64), UT(63, 192, 64), B("nm", 9, 12), A.add)
-        if up:
-            cp(B("ra", 1, 192, 64), Y(0, 192, 64))
+            f = UT(64 * c + 63, 64 * c + 64)
+            tt(at("nd", 2, 3), B(rx, 19, 20), f, A.subtract)
+            tt(at("nm", 2, 3), at("nw", m - 1, m), at("nd", 2, 3), A.mult)
+            tt(f, f, at("nm", 2, 3), A.add)
+        rows()
 
-        def strengths():
-            for c in range(3):
-                for i in sides:
-                    a, b = TS[i] + 16 * c, 16 * (at(i) + c)
-                    yield tt(own("xb", c, 63 * i - 1, 63 * i), B(tx, a, a + 16), B("mm", b, b + 16), A.subtract if i else A.add)
+    def last_meetings(p):
+        n, c = len(p), p[0]
+        tx, rx, m, l0 = "tx%d" % (3 + c), "rx%d" % (3 + c), n * len(sides), 4 * c
+        at = lambda name, a=0, b=m, w=1: B(name, w * (l0 + a), w * (l0 + b))
+        for l, i in enumerate(sides):
+            u, w = (B(rx, 19 * n, 20 * n), B(tx, 35 * n, 36 * n)) if i else (B(tx, n, 2 * n), B(rx, 17 * n, 18 * n))
+            o, r = B(tx, (2 + 16 * i) * n, (18 + 16 * i) * n), B(rx, 20 * i * n, (20 * i + 16) * n)
+            tt(at("q1", n * l, n * l + n), u, w, A.add)
+            tt(at("mc", n * l, n * l + n, 16), o if i else r, r if i else o, A.subtract)
+        ts(at("q2"), at("q1"), 8191, AND)
+        cp(at("hv"), at("q2"))
+        tt(at("mcmp", 0, m, 16), IND(EW, at("hv")), at("mc", 0, m, 16), A.is_gt)
+        mw = B("vb", 400, 400 + 16 * m)
+        mm(B("u%d" % c, 0, 16 * m), B("blk", 0, 128), at("mcmp", 0, m, 16), True, True)
+        ts(mw, B("u%d" % c, 0, 16 * m), 11.5, A.is_gt)
+        tt(at("mm", 0, m, 16), mw, at("mc", 0, m, 16), A.mult)
+        for l, i in enumerate(sides):
+            tt(B("fin", 48 * i + 16 * c, 48 * i + 16 * (c + n)), B(tx, (2 + 16 * i) * n, (18 + 16 * i) * n), at("mm", n * l, n * l + n, 16), A.subtract if i else A.add)
+        for s in range(16):
+            mm(B("w%d" % c, 0, m), B("sel", 128 * s, 128 * s + 128), B("mcmp", 16 * l0 + s, 16 * (l0 + m), 16), s == 0, s == 15)
+        ts(at("nw"), B("w%d" % c, 0, m), 11.5 * C, A.is_gt)
+        cp(at("p1"), B(rx, (17 + sides[0]) * n, (17 + sides[0]) * n + m))
+        ts(at("p2"), at("p1"), 8191, AND)
+        ts(at("p3"), at("p1"), 57344, AND)
+        ts(at("p4"), at("p2"), -4096.0, A.add, float(INV), A.mult)
+        ts(at("p1"), at("p4"), 8191, AND)
+        tt(at("pn"), at("p1"), at("p3"), A.add)
+        ys = [B("yn", 189 * i + c, 189 * i + c + n) for i in sides]
+        for l, y in enumerate(ys):
+            tt(at("nd", n * l, n * l + n), at("pn", n * l, n * l + n), y, A.subtract)
+        tt(at("nm"), at("nw"), at("nd"), A.mult)
+        for l, y in enumerate(ys):
+            tt(y, y, at("nm", n * l, n * l + n), A.add)
 
-        def held(p):
-            z, z0 = zat(p[0])
-            cols = [(at(i) + p[0], at(i) + p[-1] + 1, B(z, z0 + 62 * i + 1, z0 + 64 * len(p), 64)) for i in sides]
-            for a, b, v in cols:
-                yield tt(B("dz", a, b), B("zz", a, b), v, A.subtract)
-            for a, b, v in cols:
-                yield tt(B("zm", a, b), B("nw", a, b), B("dz", a, b), A.mult)
-            for a, b, v in cols:
-                yield tt(v, v, B("zm", a, b), A.add)
-        drain(held(PARTS[0]))
-        return chain(strengths(), held(PARTS[1]))
-
-    def decode(a, b):
-        n2, n3, ni = B("n2", a, b), B("n3", a, b), B("ni", a, b)
-        yield ts(n2, ni, 8191, AND)
-        yield ts(n3, n2, -4096.0, A.add, float(BETA), A.mult)
-        yield ts(B("wf", a, b), ni, 65535, AND)
-        yield ts(n2, n3, 8191, AND)
-        yield ts(UT(a, b), n2, float(4096 + 811 * 3), A.add)
-
-    def numbers(p):
-        a, b = 64 * p[0], 64 * p[-1] + 64
-        n1, n2, n3, ni = (B(n, a, b) for n in ("n1", "n2", "n3", "ni"))
-        yield ts(n2, ni, 8191, AND)
-        yield ts(n3, ni, 57344, AND)
-        yield ts(n1, n2, -4096.0, A.add, float(INV), A.mult)
-        yield
-        yield ts(n2, n1, 8191, AND)
-        yield
-        for c in p:
-            yield tt(B("yn", c, 192, 3), B("n2", 64 * c, 64 * c + 64), B("n3", 64 * c, 64 * c + 64), A.add)
-
-    def sources(p):
-        a, b = 64 * p[0], 64 * p[-1] + 64
-        yield cp(B("ni", a, b), ACC(a, b))
-        yield
-        yield ts(B("so", a, b), B("ni", a, b), 13, SHR, 0x7F0, AND)
-        yield
-        for c in p:
-            yield ts(B("su", c, 192, 3), B("so", 64 * c, 64 * c + 64), B("sv", c, c + 1), A.add)
-
-    n1, n2, n3 = B("n1", 0, 192), B("n2", 0, 192), B("n3", 0, 192)
-    ni, wf, ut = B("ni", 0, 192), B("wf", 0, 192), UT(0, 192)
+    n1, n2, n3, ni = (B(k, 0, 192) for k in ("n1", "n2", "n3", "ni"))
     for c in range(3):
         cp(B("n1", 64 * c, 64 * c + 64), B("bt", c, 192, 3))
     ts(n2, n1, 101.0, A.mult, 4096.0, A.add)
     ts(n3, n1, 57344, AND)
     ts(ni, n2, 8191, AND)
-    ts(n2, n1, 37.0, A.mult, 4096.0, A.add)
-    tt(wf, ni, n3, A.add)
-    ts(n3, n2, 8191, AND)
-    cp(ut, n3)
-    drain(first_list())
+    ts(UT(0, 192), n1, 37.0, A.mult, 4096.0, A.add)
+    tt(WF(0, 192), ni, n3, A.add)
+    cp(ACC(0, 192), WF(0, 192))
+    for p in PARTS:
+        columns(p, 0)
+        place_words(p)
     for c in range(3):
-        relay(c)
-        ts(B("pos", 64 * c, 64 * c + 64), B("iob", 0, 64), ONE, A.mult)
-    ts(IDN, IDP, -1.0, A.mult)
+        act(own("xa", c, -1, 63), IND(B("xn", 0, 3072), B("rl", 64 * c, 64 * c + 64)), bias=UP)
+        cp(xo(c), own("xa", c, 0, XO))
     for c in range(3):
-        first_diff("xa", c, NV0[c])
-    drain(place_words())
-    for c in range(3):
-        race_v(c, NV0[c])
-    for c in range(3):
-        cp(xo(c), own("xa", c, 0, NV[c]))
-    race_s("xa", (0, 1), 0, NV0)
-    counts(0, 0, NV0)
-    counts(1, 0, NV0)
-    race_s("xa", (2,), 0, NV0)
-    counts(2, 0, NV0)
-    later_intervals("xa")
+        races(0, c, 0)
+    later_intervals(0)
 
-    drain(post(PARTS[0], 2))
-    cp(B("ni", 0, 128), ACC(0, 128))
-    ts(B("so", 0, 128), B("ni", 0, 128), 13, SHR, 0x7F0, AND)
-    ts(B("su", 0, 128), B("so", 0, 128), B("sv", 0, 1), A.add)
-    perm(0)
-    perm(1)
-    words = decode(0, 128)
-    for _ in post(PARTS[1], 2):
-        drain(words, 1)
-    heads_and_feet(0, "xa")
-    send(0)
-    cp(B("ni", 128, 192), ACC(128, 192))
-    ts(B("so", 128, 192), B("ni", 128, 192), 13, SHR, 0x7F0, AND)
-    words = decode(128, 192)
-    drain(words, 1)
-    ts(B("su", 128, 192), B("so", 128, 192), B("sv", 0, 1), A.add)
-    drain(words, 1)
-    perm(2)
-    drain(words)
+    for p in PARTS:
+        a, b = span(p)
+        post(p, 2)
+        ts(B("su", a, b), B("so", a, b), 16.0, A.mult, B("sv", 0, 1), A.add)
+        ts(WF(a, b), B("ni", a, b), 65535, AND)
+        ts(UT(a, b), B("n2", a, b), float(BETA), A.mult, float(811 * 3 - MID), A.add)
+        place_words(p)
+        columns(p, 0)
+        for c in p:
+            send(0, (c,))
+            act(own("xb", c, -1, 63), IND(win("xa", c), B("su", 64 * c, 64 * c + 64)))
+            dma("y", xo(c), own("xb", c, 0, XO), "x%d" % c)
+    for c in range(3):
+        races(1, c, 0)
+    for c in range(3):
+        meetings(0, c)
+    later_intervals(1)
 
-    ts(B("wa", 0, 3), B("wf", 62, 192, 64), float((811 * (3 - 6)) % 8192), A.add)
-    words = place_words()
-    for _ in first_list():
-        drain(words, 1)
-    ts(B("uf", 0, 3), UT(63, 192, 64), float(811 * (6 - 3)), A.add)
-    for c in range(3):
-        first_diff("xb", c, NV1[c])
-    race_v(0, NV1[0])
-    race_v(1, NV1[1])
-    for c in range(3):
-        act(B("xe", 16 * c, 16 * c + 16), own("xb", c, 0, 1))
-        act(B("xe", 48 + 16 * c, 64 + 16 * c), own("xb", c, 61, 62))
-    race_s("xb", (0, 1), 0, NV1)
-    counts(0, 0, NV1)
-    banks = meeting(0)
-    counts(1, 0, NV1)
-    race_s("xb", (2,), 0, NV1)
-    race_v(2, NV1[2])
-    counts(2, 0, NV1)
-    for c in range(3):
-        act(xo(c), own("xb", c, 0, NV[c]))
-    later_intervals("xb", outcome(0, *banks))
-
-    drain(post(PARTS[0], 2))
-    ahead = chain(sources(PARTS[0]), numbers(PARTS[0]))
-    for _ in post(PARTS[1], 2):
-        drain(ahead, 1)
-    heads_and_feet(1, "xb")
-    send(1)
-    for _ in sources(PARTS[1]):
-        drain(ahead, 1)
+    for p in PARTS:
+        a, b = span(p)
+        post(p, 2)
+        ts(B("n3", a, b), B("ni", a, b), 57344, AND)
+        ts(B("n1", a, b), B("n2", a, b), -4096.0, A.add, float(INV), A.mult)
+        ts(B("ca", a, b), B("n1", a, b), 8191, AND)
+        for c in p:
+            ts(B("su", c, 192, 3), B("so", 64 * c, 64 * c + 64), 16.0, A.mult, B("sv", c, c + 1), A.add)
+            tt(B("yn", c, 192, 3), B("ca", 64 * c, 64 * c + 64), B("n3", 64 * c, 64 * c + 64), A.add)
+    for p in ENDS:
+        send(1, p)
     first, end = (48 if up else 0), (3024 if down else 3072)
-    for e, q, a, b in OUT:
+    lead[0] = 0.0
+    for i, (e, q, a, b) in enumerate(OUT):
         dst, src = B("outb", 16 * a, 16 * b), IND(B("xb", 0, 3 * CW), B("su", a, b))
         if e == "s":
             act(dst, src, bias=-UP)
         else:
             ts(dst, src, -UP, A.add)
         a, b = max(16 * a, first), min(16 * b, end)
-        dma(q, None, B("outb", a, b), "o1", out_ap=T.yx[:, a:b])
-    drain(ahead)
-    outcome(1, *meeting(1, numbers(PARTS[1])))
+        dma(q, T.yx[:, a:b], B("outb", a, b), "o%d" % i, 768 * i)
+    for p in ENDS:
+        last_meetings(p)
+    n = len(OUT)
     if up:
-        dma("s", None, B("fin", 0, 48), "o3", out_ap=T.yx[:, 0:48])
+        dma("s", T.yx[:, 0:48], B("fin", 0, 48), "o%d" % n)
     if down:
-        dma("y", None, B("fin", 48, 96), "o4", out_ap=T.yx[:, 3024:3072])
-    dma("y" if up else "s", None, B("yn", 0, 192), "o5", out_ap=T.yb[:])
+        dma("y", T.yx[:, 3024:3072], B("fin", 48, 96), "o%d" % (n + 1))
+    dma("y" if up else "s", T.yb[:], B("yn", 0, 192), "o%d" % (n + 2))
+
+    count, waited = {}, {}
+
+    def need(q, sem, val):
+        if waited.get((q, sem), 0) < val:
+            waited[(q, sem)] = val
+            queue[q].wait_ge(T.sem[sem], val)
+    order = in_order(calls)
+    for i in list(range(n_first)) + [i for i in order if i >= n_first]:
+        c = calls[i]
+        count[c["sem"]] = c["val"] = count.get(c["sem"], 0) + c["n"]
+        if c["call"]:
+            waits = {}
+            for j in c["after"]:
+                if not calls[j]["q"] == c["q"] == "p":
+                    waits[calls[j]["sem"]] = max(waits.get(calls[j]["sem"], 0), calls[j]["val"])
+            for sem in sorted(waits):
+                need(c["q"], sem, waits[sem])
+            done = c["call"]()
+            if c["sem"] != "loc":
+                done.then_inc(T.sem[c["sem"]], c["n"])
     for sem in sorted(count):
-        if count[sem]:
-            need("g", sem, count[sem])
+        need("g", sem, count[sem])

@@ -15,12 +15,15 @@ XO = max(NV[0][1:] + NV[1][1:])
 PIECE = 16
 OUT = (("v", "y", 0, 48), ("s", "s", 96, 144), ("v", "y", 48, 96), ("s", "s", 144, 192))
 PARTS = ((0,), (1,), (2,))
-CYCLE, GATHER, WAKE, DMA0, RATE, WAY = 0.00092, 1.5, 0.12, 1.8, 250e3, 3.8
+CYCLE, GATHER, WAKE, DMA0, RATE, WAY = 0.00088, 1.56, 0.25, 1.8, 450e3, 3.8
 ENDS = ((0, 1, 2),)
+SHORT = True
+RELAY = 5
+CROSS = 0.23
 FIRST = 1.5
 AHEAD = 0.1
 PASSES = 4
-LEAD = (2.0, 1.0, 0.0)
+LEAD = (2.5, 1.5, 0.0)
 
 
 def centred(v):
@@ -153,7 +156,7 @@ def in_order(calls):
                 if kind == "w" and v[3] == 1 and v[0] not in PSUM:
                     old[:] = [e for e in old if not (v[1] <= e[1][1] and e[1][2] <= v[2])]
                 old.append((kind, v, i))
-    gap = lambda j, i: 0.0 if calls[j]["q"] == calls[i]["q"] == "p" else WAKE
+    gap = lambda j, i: CROSS if calls[j]["q"] != calls[i]["q"] else 0.0 if calls[i]["q"] == "p" else WAKE
     for c in calls:
         c["way"], c["next"] = c["time"], []
     for i in reversed(range(len(calls))):
@@ -275,7 +278,7 @@ def rank_program(g, core, T, topo):
     def gsel(out, a, pattern, cmpop, val, base, cm):
         op("g", [a], [out], lambda: g.affine_select(ap(out), ap(a), pattern, cmpop, val, base, cm))
 
-    dma("y", B("bt", 0, 192), T.boat[:], "db")
+    dma("y", B("bt", 0, 192), T.boat[:], "db", 3072)
     dma("s", B("xn", 0, 3072), T.x[:], "dx")
     dma("y", EW, T.enc[:], "de", 3072)
     dma("y", B("ew", 8192, 8192 + WRAP), T.enc[:, 0:WRAP], "dw", 3072 + 8192)
@@ -307,9 +310,8 @@ def rank_program(g, core, T, topo):
         fill(B(k, 0, 1), -float(2 ** 30))
         fill(B(k, 1, 1 + n), -11.5 * C)
         fill(B(k, 1 + n, 64), -7.0 * C)
-    ts(B("blc", 0, 128), B("jb", 0, 128), 0.0, A.is_ge, C, A.mult)
     for s in range(16):
-        gsel(B("sel", 128 * s, 128 * s + 128), B("blc", 0, 128), [[0, 8], [1, 16]], A.is_equal, 0.0, -s, 0)
+        ts(B("sel", 128 * s, 128 * s + 128), B("jb", 0, 128), float(s), A.is_equal, C, A.mult)
     ts(B("blk", 0, 128), B("jb", 0, 128), 0.0, A.is_ge)
     ts(IDN, IDP, -1.0, A.mult)
     for c in range(3):
@@ -377,8 +379,13 @@ def rank_program(g, core, T, topo):
             ts(B("so", a, b), ACC(a, b), 1 / ONE, A.mult, -0.25, A.add)
             ts(B("n2", a, b), B("ni", a, b), 8191, AND)
             return
-        tt(x, nbx, s, A.max)
-        tt(Y(a, b), Y(a, b), x, A.subtract)
+        if SHORT:
+            ts(x, s, 0.0, A.max)
+            tt(ys, Y(a, b), x, A.subtract)
+            tt(Y(a, b), ys, nbx, A.subtract)
+        else:
+            tt(x, nbx, s, A.max)
+            tt(Y(a, b), Y(a, b), x, A.subtract)
         scan(R(a + 1, b), B("rst", a, b - 1), Y(a, b - 1), 0.0, A.mult, A.max)
         ts(B(M(k + 1), a, b), Y(a, b), 0.0, A.is_le, HUGE, A.mult)
         ts(B("oi", a, b - 1), R(a + 1, b), 1 / ONE, A.mult, -0.25, A.add)
@@ -540,7 +547,10 @@ def rank_program(g, core, T, topo):
         columns(p, 0)
         place_words(p)
     for c in range(3):
-        act(own("xa", c, -1, 63), IND(B("xn", 0, 3072), B("rl", 64 * c, 64 * c + 64)), bias=UP)
+        if c == RELAY:
+            ts(own("xa", c, -1, 63), IND(B("xn", 0, 3072), B("rl", 64 * c, 64 * c + 64)), UP, A.add)
+        else:
+            act(own("xa", c, -1, 63), IND(B("xn", 0, 3072), B("rl", 64 * c, 64 * c + 64)), bias=UP)
         cp(xo(c), own("xa", c, 0, XO))
     for c in range(3):
         races(0, c, 0)

@@ -7,23 +7,23 @@ AND = A.bitwise_and
 C = float(2 ** 25)
 HUGE = float(2 ** 60)
 ONE = 131072.0
+MORE = 16000000
+BIG = 1024.0
 UP = 128.0
 CW = 1040
 WRAP = 1632
-NV = ((32, 26, 26), (20, 26, 30))
-XO = max(NV[0][1:] + NV[1][1:])
+NV = (((40, 32, 20), (26, 26, 26), (26, 26, 26)), ((36, 24, 14), (26, 26, 26), (30, 30, 30)))
+XO = max(_n for _d in NV for _k in _d[1:] for _n in _k)
+NA = 50
 PIECE = 16
+RELAY = (1,)
+SELG = 8
 OUT = (("v", "y", 0, 48), ("s", "s", 96, 144), ("v", "y", 48, 96), ("s", "s", 144, 192))
-PARTS = ((0,), (1,), (2,))
-CYCLE, GATHER, WAKE, DMA0, RATE, WAY = 0.00088, 1.56, 0.25, 1.8, 450e3, 3.8
-ENDS = ((0, 1, 2),)
-SHORT = True
-RELAY = 5
-CROSS = 0.23
-FIRST = 1.5
-AHEAD = 0.1
-PASSES = 4
-LEAD = (2.5, 1.5, 0.0)
+CYCLE, GATHER, WAKE, CROSS, DMA0, RATE, WAY, FIRST = 0.00088, 1.56, 0.25, 0.23, 1.8, 550e3, 3.8, 1.5
+AHEAD = 0.05
+LEADS = ((2.0, 1.0, 0.0), (2.5, 1.5, 0.0), (3.0, 1.5, 0.0), (1.5, 1.0, 0.0))
+LEAD = (0, 1, 2)
+PASSES = 3
 
 
 def centred(v):
@@ -37,31 +37,29 @@ MID = 8192 * 600
 
 F, H, I, U = "float32", "bfloat16", "int32", "uint16"
 SCRATCH = {}
-for _n, _w, _t in (("xn", 3072, H), ("outb", 3072, H), ("ew", 8192 + WRAP, H), ("bt", 192, I), ("xa", 3 * CW, H), ("xb", 3 * CW, H), ("sel", 2048, H),
-                   ("jb0", 128, H), ("jb1", 128, H), ("jb", 128, H), ("one", 128, H), ("idp", 128, H), ("idn", 128, H), ("blk", 128, H), ("blc", 128, H),
-                   ("pi", 1, I), ("pj", 1, I), ("sv", 8, F), ("io48", 64, I), ("iob", 64, I),
-                   ("zero", 192, H), ("rst", 192, H), ("neg", 192, H), ("rl", 192, U), ("n1", 192, I), ("n2", 192, I), ("n3", 192, I),
-                   ("uw", 384, I), ("ni", 192, I), ("so", 192, I), ("su", 192, U), ("hu", 6, U), ("hv", 12, U),
-                   ("q1", 12, I), ("q2", 12, I), ("mc", 192, F), ("mm", 192, F), ("mcmp", 192, H), ("mw", 192, F), ("fin", 96, H),
-                   ("nd", 12, F), ("nw", 12, F), ("nm", 12, F), ("zz", 12, F), ("dz", 12, F), ("zm", 12, F), ("ow", 12, F),
-                   ("pn", 12, F), ("p1", 12, I), ("p2", 12, I), ("p3", 12, I), ("p4", 12, I), ("yn", 192, F), ("xo", 48 * XO, H),
-                   ("s", 192, F), ("vt", 192, F), ("xk", 192, F), ("t", 192, F), ("nk", 192, F), ("ys", 192, F), ("ma", 192, H), ("mb", 192, H),
-                   ("cs", 192, I), ("ca", 192, I), ("oi", 192, I), ("cu", 192, U), ("of", 192, U)):
+for _n, _w, _t in (("xn", 3072, H), ("outb", 3072, H), ("ew", 8192 + WRAP, H), ("bt", 192, I), ("xa", 3 * CW, H), ("xb", 3 * CW, H), ("xo", 48 * XO, H),
+                   ("sel", 2048, H), ("jb0", 128, H), ("jb1", 128, H), ("jb", 128, H), ("one", 128, H), ("idp", 128, H), ("idn", 128, H),
+                   ("blk", 128, H), ("blc", 128, H), ("blp", 128, H), ("bln", 128, H), ("k0", 126, H), ("k1", 126, H), ("kg", 96, H), ("kz", 4, H), ("neg", 64, H),
+                   ("pi", 1, I), ("pj", 1, I), ("pf", 1, F), ("sv", 3, F), ("ioc", 3, I), ("iol", 192, I), ("iob", 64, I), ("rl", 192, U),
+                   ("n1", 192, I), ("n2", 192, I), ("n3", 192, I), ("uw", 384, I), ("ni", 192, I), ("so", 192, I), ("su", 192, U), ("yn", 192, F),
+                   ("s0", 195, F), ("x0", 195, F), ("s", 192, F), ("vt", 192, F), ("xk", 192, F), ("t", 192, F), ("nk", 192, F), ("ys", 192, F),
+                   ("ma", 192, H), ("mb", 192, H), ("cs", 192, I), ("ca", 192, I), ("oi", 192, I), ("cu", 192, U), ("of", 192, U),
+                   ("hu", 6, U), ("hv", 12, U), ("q1", 12, I), ("q2", 12, I), ("mc", 192, F), ("mm", 192, F), ("mcmp", 192, H), ("mw", 192, F),
+                   ("nd", 12, F), ("nw", 12, F), ("nn", 12, F), ("nm", 12, F), ("zz", 12, F), ("ow", 12, F), ("p1", 6, I), ("p4", 6, I),
+                   ("fa", 96, F), ("fin", 96, H)):
     SCRATCH[_n] = ("sbuf", [128, _w], _t)
 for _c in range(3):
     for _n in ("dv", "cmp", "xr", "es"):
         SCRATCH["%s_%d" % (_n, _c)] = ("sbuf", [128, 1008], H)
-for _c in range(6):
-    SCRATCH["tx%d" % _c] = SCRATCH["rx%d" % _c] = ("sbuf", [128, 108], F)
-for _c in sorted(set(NV[0] + NV[1])):
-    SCRATCH["kc%d" % _c] = ("sbuf", [128, 64], H)
+for _c in range(4):
+    SCRATCH["tx%d" % _c] = SCRATCH["rx%d" % _c] = ("sbuf", [128, 36 if _c < 3 else 114], F)
 PSUM = ("va", "vb", "u0", "u1", "u2", "w0", "w1", "w2")
-Z = 320
+Z = 448
 for _n in PSUM:
     SCRATCH[_n] = ("psum", [128, 512], F)
 QSEM = {"v": "qv", "s": "qs", "p": "qp", "g": "qg"}
-SEMAPHORES = (["qv", "qs", "qp", "qg", "db", "dx", "de", "dw", "x0", "x1", "x2", "loc"] + ["o%d" % _c for _c in range(len(OUT) + 3)]
-              + ["r%s%d" % (_n, _c) for _n in "hf" for _c in range(6)])
+SEMAPHORES = (["qv", "qs", "qp", "qg", "db", "dx", "de", "dw", "loc"] + ["x%d" % _c for _c in range(6)] + ["o%d" % _c for _c in range(len(OUT) + 3)]
+              + ["r%s%d" % (_n, _c) for _n in "hf" for _c in range(4)])
 
 
 def B(name, a, b, step=1):
@@ -83,7 +81,7 @@ def size(v):
 def meet(v, w):
     if v[0] != w[0] or v[1] >= w[2] or w[1] >= v[2]:
         return False
-    return v[3] != w[3] or (v[1] - w[1]) % v[3] == 0
+    return abs(v[3]) == abs(w[3]) == 1 or not set(range(v[1], v[2], abs(v[3]))).isdisjoint(range(w[1], w[2], abs(w[3])))
 
 
 def own(x, c, j0, j1, shift=0):
@@ -99,27 +97,18 @@ def xo(c, j0=0, j1=XO):
     return B("xo", 16 * (c * XO + j0), 16 * (c * XO + j1))
 
 
-def Y(a, b, step=1):
-    return B("va", a, b, step)
+LISTS = {"Y": ("va", 0, 64), "ACC": ("va", 192, 64), "R": ("vb", 0, 64), "NB": ("vb", 192, 65), "UT": ("uw", 0, 64), "WF": ("uw", 192, 64),
+         "s0": ("s0", 0, 65), "x0": ("x0", 0, 65)}
 
 
-def ACC(a, b, step=1):
-    return B("va", 192 + a, 192 + b, step)
+def L(name, c, a=0, b=64, step=1):
+    buf, first, stride = LISTS.get(name, (name, 0, 64))
+    return B(buf, first + stride * c + a, first + stride * c + b, step)
 
 
-POS = B("va", 384, 448)
-
-
-def R(a, b):
-    return B("vb", a, b)
-
-
-def UT(a, b, step=1):
-    return B("uw", a, b, step)
-
-
-def WF(a, b, step=1):
-    return B("uw", 192 + a, 192 + b, step)
+def ends(name, i):
+    buf, first, stride = LISTS.get(name, (name, 0, 64))
+    return B(buf, first + 63 * i, first + 3 * stride, stride)
 
 
 def M(k):
@@ -130,16 +119,13 @@ def t_(n, c, a, b, step=1):
     return B("%s_%d" % (n, c), a, b, step)
 
 
-def span(p):
-    return 64 * p[0], 64 * p[-1] + 64
+def Zc(c, a=1, b=64, step=1):
+    return B("w%d" % c, Z + a, Z + b, step)
 
 
-def zat(c):
-    return "w%d" % [p[0] for p in PARTS if c in p][0], Z + 64 * c
-
-
+POS = B("va", 384, 448)
 EW, EWX = B("ew", 0, 8192), B("ew", 0, 8192 + WRAP)
-IDP, IDN = B("idp", 0, 128), B("idn", 0, 128)
+IDP, IDN, SV0 = B("idp", 0, 128), B("idn", 0, 128), B("sv", 0, 1)
 
 
 def in_order(calls):
@@ -163,23 +149,25 @@ def in_order(calls):
         for j in calls[i]["after"]:
             calls[j]["way"] = max(calls[j]["way"], calls[j]["time"] + gap(j, i) + calls[i]["way"])
             calls[j]["next"].append(i)
-    free, order = {}, []
-    left = [len(c["after"]) for c in calls]
-    ready = {i: 0.0 for i in range(len(calls)) if not left[i]}
-    while ready:
-        start = {i: max(t, free.get(calls[i]["q"], 0.0)) for i, t in ready.items()}
-        first = min(start, key=lambda i: (start[i], i))
-        q = calls[first]["q"]
-        i = max((i for i in start if calls[i]["q"] == q and start[i] <= start[first] + AHEAD), key=lambda i: (calls[i]["way"] + calls[i]["lead"] - start[i], -i))
-        c = calls[i]
-        del ready[i]
-        free[q] = start[i] + c["hold"]
-        c["end"] = start[i] + c["time"]
-        order.append(i)
-        for j in c["next"]:
-            left[j] -= 1
-            if not left[j]:
-                ready[j] = max(calls[k]["end"] + gap(k, j) for k in calls[j]["after"])
+
+    def longest_first(lead):
+        free, order, end = {}, [], {}
+        left = [len(c["after"]) for c in calls]
+        ready = {i: 0.0 for i in range(len(calls)) if not left[i]}
+        while ready:
+            start = {i: max(t, free.get(calls[i]["q"], 0.0)) for i, t in ready.items()}
+            first = min(start, key=lambda i: (start[i], i))
+            q = calls[first]["q"]
+            i = max((i for i in start if calls[i]["q"] == q and start[i] <= start[first] + AHEAD),
+                    key=lambda i: (calls[i]["way"] + lead[calls[i]["chunk"]] - start[i], -i))
+            del ready[i]
+            free[q], end[i] = start[i] + calls[i]["hold"], start[i] + calls[i]["time"]
+            order.append(i)
+            for j in calls[i]["next"]:
+                left[j] -= 1
+                if not left[j]:
+                    ready[j] = max(end[k] + gap(k, j) for k in calls[j]["after"])
+        return order
 
     def place(order, behind):
         t, busy = {}, {}
@@ -196,13 +184,15 @@ def in_order(calls):
         return t
     forth = [[(j, calls[j]["time"] + gap(j, i)) for j in c["after"]] for i, c in enumerate(calls)]
     back = [[(j, calls[j]["hold"] + gap(i, j) + c["time"] - c["hold"]) for j in c["next"]] for i, c in enumerate(calls)]
-    best = (max(c["end"] for c in calls), order)
-    for _ in range(PASSES):
-        t = place(order[::-1], back)
-        order = sorted(order, key=lambda i: -t[i] - calls[i]["hold"])
-        t = place(order, forth)
-        order = sorted(order, key=lambda i: t[i])
-        best = min(best, (max(t[i] + calls[i]["time"] for i in order), order))
+    best = (1e9, None)
+    for lead in LEADS:
+        order = longest_first(lead)
+        for _ in range(PASSES):
+            t = place(order[::-1], back)
+            order = sorted(order, key=lambda i: -t[i] - calls[i]["hold"])
+            t = place(order, forth)
+            order = sorted(order, key=lambda i: t[i])
+            best = min(best, (max(t[i] + calls[i]["time"] for i in order), order))
     return best[1]
 
 
@@ -212,8 +202,9 @@ def rank_program(g, core, T, topo):
         return
     n_ranks = len(T.cores)
     up, down = rank > 0, rank < n_ranks - 1
+    sides = [i for i, ok in ((0, up), (1, down)) if ok]
     queue = {"v": g.vector, "s": g.scalar, "p": g.tensor, "g": g, "y": g.sync}
-    calls, lead = [], [0.0]
+    calls, lead = [], [2]
 
     def ap(v):
         if not isinstance(v, tuple):
@@ -228,7 +219,7 @@ def rank_program(g, core, T, topo):
     def note(q, reads, writes, call, time, hold=None, sem=None, n=1, after=()):
         flat = lambda views: [e for v in views if isinstance(v, tuple) for e in entries(v)]
         calls.append({"q": q, "reads": flat(reads), "writes": flat(writes), "call": call, "time": time, "hold": time if hold is None else hold,
-                      "lead": lead[0], "sem": sem or QSEM[q], "n": n, "after": after})
+                      "chunk": lead[0], "sem": sem or QSEM[q], "n": n, "after": after})
         return len(calls) - 1
 
     def op(q, reads, writes, call, cycles=None):
@@ -268,65 +259,80 @@ def rank_program(g, core, T, topo):
     def mm(out, lhs, rhs, start, stop):
         op("p", [lhs, rhs], [out], lambda: g.tensor.matmul(ap(out), ap(lhs), ap(rhs), start, stop))
 
-    def dma(q, out, a, sem, before=0):
+    def dma(q, out, a, sem, before=0, behind=()):
         n = 256 * (before + size(out if isinstance(out, tuple) else a))
-        note(q, [a], [out], lambda: queue[q].dma_start(ap(out), ap(a)), DMA0 + n / RATE, 0.05, sem, 16)
+        note(q, [a, *behind], [out], lambda: queue[q].dma_start(ap(out), ap(a)), DMA0 + n / RATE, 0.05, sem, 16)
 
-    def gi(out, pattern, base, cm, **kw):
+    def gi(out, pattern, base, cm):
+        kw = {} if SCRATCH[out[0]][2] == I else {"allow_small_or_imprecise_dtypes": True}
         op("g", [], [out], lambda: g.iota(ap(out), pattern, base, cm, **kw))
+
+    def gfill(out, val):
+        gi(out, [[0, size(out)]], val, 0)
 
     def gsel(out, a, pattern, cmpop, val, base, cm):
         op("g", [a], [out], lambda: g.affine_select(ap(out), ap(a), pattern, cmpop, val, base, cm))
 
+    def gather(e, out, src, add):
+        if e == "s":
+            act(out, src, bias=add)
+        else:
+            ts(out, src, add, A.add)
+
     dma("y", B("bt", 0, 192), T.boat[:], "db", 3072)
     dma("s", B("xn", 0, 3072), T.x[:], "dx")
     dma("y", EW, T.enc[:], "de", 3072)
-    dma("y", B("ew", 8192, 8192 + WRAP), T.enc[:, 0:WRAP], "dw", 3072 + 8192)
     n_first = len(calls)
+    dma("y", B("ew", 8192, 8192 + WRAP), T.enc[:, 0:WRAP], "dw", 0, [EW])
 
     gi(B("pi", 0, 1), [[0, 1]], 0, 1)
-    gi(B("io48", 0, 64), [[48, 64]], 0, 0)
+    gi(B("iol", 0, 192), [[16, 3], [48, 64]], 0, 0)
+    gi(B("ioc", 0, 3), [[CW, 3]], 0, 0)
     gi(B("iob", 0, 64), [[1, 64]], 1, 0)
-    gi(B("jb0", 0, 128), [[0, 8], [1, 16]], 0, 0, allow_small_or_imprecise_dtypes=True)
+    gi(B("jb0", 0, 128), [[0, 8], [1, 16]], 0, 0)
     fill(B("one", 0, 128), 1.0)
     gsel(B("jb1", 0, 128), B("jb0", 0, 128), [[-16, 8], [0, 16]], A.is_ge, -1.0, 0, 1)
     gsel(B("jb", 0, 128), B("jb1", 0, 128), [[16, 8], [0, 16]], A.is_ge, -1.0, 15, -1)
     gsel(IDP, B("one", 0, 128), [[-1, 128]], A.is_equal, 0.0, 0, 1)
-    ts(B("pj", 0, 1), B("pi", 0, 1), 15, AND)
-    for c in range(3):
-        ts(B("sv", 4 + c, 5 + c), B("pj", 0, 1), float(16 * c), A.add)
-        ts(B("rl", 64 * c, 64 * c + 64), B("io48", 0, 64), B("sv", 4 + c, 5 + c), A.add)
-        ts(B("sv", c, c + 1), B("pj", 0, 1), float(CW * c), A.add)
-    for n, v in (("zero", 0.0), ("rst", 1.0), ("neg", -1.0), ("t", 0.0)):
-        fill(B(n, 0, 192), v)
-    fill(B("rst", 0, 192, 64), 0.0)
-    fill(B("vb", 0, 400), 0.0)
-    ts(POS, B("iob", 0, 64), ONE, A.mult)
-    for c in range(3):
-        fill(B("xa", c * CW, c * CW + 16), 512.0)
-        fill(B("xb", c * CW, c * CW + 16), 512.0)
-    for n in sorted(set(NV[0] + NV[1])):
-        k = "kc%d" % n
-        fill(B(k, 0, 1), -float(2 ** 30))
-        fill(B(k, 1, 1 + n), -11.5 * C)
-        fill(B(k, 1 + n, 64), -7.0 * C)
-    for s in range(16):
-        ts(B("sel", 128 * s, 128 * s + 128), B("jb", 0, 128), float(s), A.is_equal, C, A.mult)
-    ts(B("blk", 0, 128), B("jb", 0, 128), 0.0, A.is_ge)
     ts(IDN, IDP, -1.0, A.mult)
+    ts(B("pj", 0, 1), B("pi", 0, 1), 15, AND)
+    cp(B("pf", 0, 1), B("pj", 0, 1))
+    ts(B("rl", 0, 192), B("iol", 0, 192), B("pf", 0, 1), A.add)
+    ts(B("sv", 0, 3), B("ioc", 0, 3), B("pf", 0, 1), A.add)
+    ts(POS, B("iob", 0, 64), ONE, A.mult)
+    fill(B("neg", 0, 64), -1.0)
+    fill(ends("R", 0), 0.0)
+    fill(B("vb", 256, 387, 65), 0.0)
+    gfill(B("s0", 0, 195), MORE)
+    gfill(B("x0", 0, 195), 0)
+    gfill(B("s", 0, 192), -1)
+    for x in ("xa", "xb"):
+        for c in range(3):
+            gfill(B(x, c * CW, c * CW + 16), 512)
+    for k, v, s in (("k0", -4.5, 7.0), ("k1", -11.5, -7.0)):
+        fill(B(k, 0, 63), v * C)
+        fill(B(k, 63, 126), s * C)
+    ts(B("blc", 0, 128), B("jb", 0, 128), 0.0, A.is_ge, C, A.mult)
+    for s in range(16):
+        if s < SELG:
+            gsel(B("sel", 128 * s, 128 * s + 128), B("blc", 0, 128), [[0, 8], [1, 16]], A.is_equal, 0.0, -s, 0)
+        else:
+            ts(B("sel", 128 * s, 128 * s + 128), B("jb", 0, 128), float(s), A.is_equal, C, A.mult)
+    for k, v in (("blk", 1.0), ("blp", BIG), ("bln", -BIG)):
+        ts(B(k, 0, 128), B("jb", 0, 128), 0.0, A.is_ge, v, A.mult)
+    gfill(B("kg", 0, 96), int(11.5 * BIG))
+    fill(B("kz", 0, 4), -11.5 * C)
     for c in range(3):
-        fill(B("tx%d" % c, 34, 35), 0.0)
-    for p in ENDS:
-        fill(B("tx%d" % (3 + p[0]), 34 * len(p), 35 * len(p)), 0.0)
+        gfill(B("tx%d" % c, 34, 35), 0)
+    gfill(B("tx3", 105, 108), 0)
 
-    def columns(p, k):
-        a, b = span(p)
-        tt(B("cs", a, b - 1), UT(a + 1, b), R(a + 1, b) if k else ACC(a, b - 1), A.add)
-        ts(B("ca", a, b - 1), B("cs", a, b - 1), 8191, AND)
-        ts(B("cu", a, b - 1), B("ca", a, b - 1), float(811 * k), A.add)
+    def columns(c, k):
+        tt(L("cs", c, 0, 63), L("UT", c, 1), L("R", c, 1) if k else L("ACC", c, 0, 63), A.add)
+        ts(L("ca", c, 0, 63), L("cs", c, 0, 63), 8191, AND)
+        ts(L("cu", c, 0, 63), L("ca", c, 0, 63), float(811 * k), A.add)
 
     def races(day, c, k):
-        x, nv, ew = "xb" if day else "xa", NV[day][k], EWX if k else EW
+        x, nv, ew = "xb" if day else "xa", NV[day][k][c], EWX if k else EW
         lead[0] = LEAD[c]
         if not k:
             scan(t_("dv", c, 0, 16 * nv), own(x, c, 0, nv, -1), own(x, c, 0, nv), 0.0, A.max, A.subtract)
@@ -334,95 +340,74 @@ def rank_program(g, core, T, topo):
             j1 = min(j0 + PIECE, nv)
             dv = t_("dv", c, 16 * j0, 16 * j1)
             if k:
-                tt(dv, IND(win(x, c), B("of", 64 * c + j0, 64 * c + j1)), xo(c, j0, j1), A.subtract)
-            tt(t_("cmp", c, 16 * j0, 16 * j1), IND(ew, B("cu", 64 * c + j0, 64 * c + j1)), dv, A.is_gt)
-        na = max(nv + 2 * ((66 - nv) // 4), 44)
+                tt(dv, IND(win(x, c), L("of", c, j0, j1)), xo(c, j0, j1), A.subtract)
+            tt(t_("cmp", c, 16 * j0, 16 * j1), IND(ew, L("cu", c, j0, j1)), dv, A.is_gt if k else A.is_le)
+        na = min(nv + 32, NA)
         for u, j0, j1 in (("u", nv, na), ("w", na, 63)):
             o = B("%s%d" % (u, c), 0, 16 * (j1 - j0))
             xr, es = t_("xr", c, 16 * j0, 16 * j1), t_("es", c, 16 * j0, 16 * j1)
             mm(o, IDP, own(x, c, j0, j1), True, False)
             if k:
-                act(xr, IND(win(x, c), B("of", 64 * c + j0, 64 * c + j1)))
+                act(xr, IND(win(x, c), L("of", c, j0, j1)))
             mm(o, IDN, xr if k else own(x, c, j0, j1, -1), False, False)
-            act(es, IND(ew, B("cu", 64 * c + j0, 64 * c + j1)))
+            act(es, IND(ew, L("cu", c, j0, j1)))
             mm(o, IDP, es, False, True)
-            act(t_("cmp", c, 16 * j0, 16 * j1), o, ACT.Sign, bias=-0.5)
-        z, a = zat(c)
-        mm(B(z, a, a + 64), IDP, B("kc%d" % nv, 0, 64), True, False)
+            act(t_("cmp", c, 16 * j0, 16 * j1), o, ACT.Sign, bias=-0.5 if k else 0.5, scale=1.0 if k else -1.0)
+        mm(Zc(c), IDP, B("k1" if k else "k0", 63 - nv, 126 - nv), True, False)
         if k:
-            mm(B(z, a + 1, a + 64), IDP, B(M(k), 64 * c + 1, 64 * c + 64), False, False)
+            mm(Zc(c), IDP, L(M(k), c, 1), False, False)
         for s in range(16):
-            mm(B(z, a + 1, a + 64), B("sel", 128 * s, 128 * s + 128), t_("cmp", c, s, 1008, 16), False, s == 15)
+            mm(Zc(c), B("sel", 128 * s, 128 * s + 128), t_("cmp", c, s, 1008, 16), False, s == 15)
 
-    def post(p, k):
-        a, b = span(p)
-        lead[0] = LEAD[p[0]]
-        o = 192 + a + PARTS.index(p)
-        nbr, nbx = B("vb", o, o + b - a, -1), B("vb", o + 1, o + 1 + b - a)
-        s, vt, t, x, nk, ys = (B(i, a, b) for i in ("s", "vt", "t", "xk", "nk", "ys"))
-        scan(s, B("neg", a, b), B(zat(p[0])[0], Z + a, Z + b), -1.0, A.mult, A.min)
-        tt(vt, Y(a, b), s, A.min)
-        scan(nbr, B(M(k) if k else "zero", a, b, -1), B("vt", a, b, -1), 0.0, A.min, A.max)
-        if k:
-            tt(t, R(a, b), vt, A.min)
-            tt(ACC(a, b), ACC(a, b), t, A.max)
-            tt(nk, nbx, B(M(k), a, b), A.subtract)
+    def post(c, k):
+        lead[0] = LEAD[c]
+        Y, ACC, R, s, vt, t, x, nk, ys = (L(i, c) for i in ("Y", "ACC", "R", "s", "vt", "t", "xk", "nk", "ys"))
+        neg, nbx = B("neg", 0, 63), L("NB", c, 1, 65)
+        if not k:
+            scan(L("s0", c, 1), neg, Zc(c), C, A.mult, A.max)
+            tt(Y, L("NB", c), L("s0", c), A.min)
+            tt(Y, Y, L("s0", c, 1, 65), A.min)
+            ts(L("x0", c), L("s0", c), -1.0, A.mult, 0.0, A.max)
+            tt(ACC, nbx, L("x0", c, 1, 65), A.min)
+            tt(L("t", c, 1), L("NB", c, 0, 63), L("x0", c, 1), A.min)
+            tt(L("ACC", c, 1), L("ACC", c, 1), L("t", c, 1), A.max)
         else:
-            tt(B("t", a + 1, b), Y(a, b - 1), B("vt", a + 1, b), A.min)
-            tt(ACC(a, b), nbx, t, A.max)
+            scan(L("s", c, 1), neg, Zc(c), -C, A.mult, A.min)
+            tt(vt, Y, s, A.min)
+            scan(L("NB", c, 0, 64, -1), L(M(k), c, 0, 64, -1), L("vt", c, 0, 64, -1), 0.0, A.min, A.max)
+            ts(x, s, 0.0, A.max)
+            tt(ys, Y, x, A.subtract)
+            tt(nk, nbx, L(M(k), c), A.subtract)
+        if k == 1:
+            tt(Y, ys, nbx, A.subtract)
+            tt(t, R, vt, A.min)
+            tt(ACC, ACC, t, A.max)
+            tt(ACC, ACC, nk, A.max)
         if k == 2:
-            ts(x, s, 0.0, A.max)
-            tt(ys, Y(a, b), x, A.subtract)
-            tt(ACC(a, b), ACC(a, b), ys, A.max)
-            tt(ACC(a, b), ACC(a, b), nk, A.max)
-            cp(B("ni", a, b), ACC(a, b))
-            ts(B("so", a, b), ACC(a, b), 1 / ONE, A.mult, -0.25, A.add)
-            ts(B("n2", a, b), B("ni", a, b), 8191, AND)
+            tt(ACC, ACC, ys, A.max)
+            tt(ACC, ACC, nk, A.max)
+            cp(L("ni", c), ACC)
+            ts(L("so", c), ACC, 1 / ONE, A.mult, -0.25, A.add)
+            ts(L("n2", c), L("ni", c), 8191, AND)
             return
-        if SHORT:
-            ts(x, s, 0.0, A.max)
-            tt(ys, Y(a, b), x, A.subtract)
-            tt(Y(a, b), ys, nbx, A.subtract)
-        else:
-            tt(x, nbx, s, A.max)
-            tt(Y(a, b), Y(a, b), x, A.subtract)
-        scan(R(a + 1, b), B("rst", a, b - 1), Y(a, b - 1), 0.0, A.mult, A.max)
-        ts(B(M(k + 1), a, b), Y(a, b), 0.0, A.is_le, HUGE, A.mult)
-        ts(B("oi", a, b - 1), R(a + 1, b), 1 / ONE, A.mult, -0.25, A.add)
-        ts(B("of", a, b - 1), B("oi", a, b - 1), 16.0, A.mult, B("sv", 0, 1), A.add)
-        columns(p, k + 1)
+        scan(L("R", c, 1), neg, L("Y", c, 0, 63), 0.0, A.max, A.max)
+        ts(L(M(k + 1), c), Y, 0.0, A.is_le, HUGE, A.mult)
+        ts(L("oi", c, 0, 63), L("R", c, 1), 1 / ONE, A.mult, -0.25, A.add)
+        ts(L("of", c, 0, 63), L("oi", c, 0, 63), 16.0, A.mult, SV0, A.add)
+        columns(c, k + 1)
         if k:
-            tt(ACC(a, b), ACC(a, b), nk, A.max)
+            tt(t, R, L(M(2), c), A.subtract)
+            tt(ACC, ACC, t, A.max)
 
     def later_intervals(day):
         for k in range(2):
-            for p in PARTS:
-                post(p, k)
             for c in range(3):
+                post(c, k)
                 races(day, c, k + 1)
 
-    def place_words(p):
-        for c in p:
-            tt(Y(64 * c, 64 * c + 64), POS, WF(64 * c, 64 * c + 64), A.add)
-
-    sides = [i for i, ok in ((0, up), (1, down)) if ok]
-
-    def send(day, p):
-        m, n, (a, b) = 3 * day + p[0], len(p), span(p)
-        tx, rx, hu, w = "tx%d" % m, "rx%d" % m, B("hu", 2 * p[0], 2 * p[0] + 2 * n), 18 * n
-        for j, c in enumerate(p):
-            ts(B("hu", 2 * p[0] + j, 2 * p[0] + 2 * n, n), B("so", 64 * c, 64 * c + 64, 63), 16.0, A.mult, B("sv", j, j + 1), A.add)
-        src = IND(B("xb" if day else "xa", p[0] * CW, (p[-1] + 1) * CW), hu)
-        if day:
-            ts(B(tx, 2 * n, 34 * n), src, -UP, A.add)
-        else:
-            cp(B(tx, 2 * n, 34 * n), src)
-        if n == 1:
-            cp(B(tx, 0, 36, 35), (ACC if day else WF)(a, b, 63))
-        else:
-            for i in range(2):
-                cp(B(tx, 35 * n * i, 35 * n * i + n), ACC(a + 63 * i, b, 64))
-        ts(B(tx, n, 2 * n), B("n2", a, b, 64), float(BETA), A.mult, float(811 * (7 if day else 3) - MID), A.add)
+    def message(m):
+        tx, rx = "tx%d" % m, "rx%d" % m
+        w = SCRATCH[tx][1][1] // 2
         ways = ([(rank - 1, 0, w, "rh%d" % m)] if up else []) + ([(rank + 1, w, 0, "rf%d" % m)] if down else [])
         trs, n = [], 0
         for i, (r, a, b, sem) in enumerate(ways):
@@ -438,165 +423,138 @@ def rank_program(g, core, T, topo):
                 fan = (1 if r > 0 else 0) + (1 if r < n_ranks - 1 else 0)
                 note(sem, [], [B(rx, a, a + w)], None, WAY + (0 if m else FIRST), 0.0, sem, len(topo.engines(T.cores[r], core)) // fan, [sent])
 
-    def meetings(day, c):
-        lead[0] = LEAD[c]
-        tx, rx, u, m = "tx%d" % (3 * day + c), "rx%d" % (3 * day + c), "u%d" % c, len(sides)
-        lb = m if day else 2 * m
+    def places(c, out, base):
+        ts(out, L("so", c, 0, 64, 63), 16.0, A.mult, base, A.add)
+
+    def night(c):
+        tx, hu = "tx%d" % c, B("hu", 2 * c, 2 * c + 2)
+        ts(L("su", c), L("so", c), 16.0, A.mult, SV0, A.add)
+        ts(L("WF", c), L("ni", c), 65535, AND)
+        ts(L("UT", c), L("n2", c), float(BETA), A.mult, float(811 * 3 - MID), A.add)
+        tt(L("NB", c), POS, L("WF", c), A.add)
+        columns(c, 0)
+        places(c, hu, SV0)
+        cp(B(tx, 2, 34), IND(win("xa", c), hu))
+        cp(B(tx, 0, 36, 35), L("WF", c, 0, 64, 63))
+        ts(B(tx, 1, 2), L("n2", c, 0, 1), float(BETA), A.mult, float(811 * 3 - MID), A.add)
+        message(c)
+        for j in (0, 32):
+            act(own("xb", c, j - 1, j + 31), IND(win("xa", c), L("su", c, j, j + 32)))
+        dma("y", xo(c), own("xb", c, 0, XO), "x%d" % (3 + c))
+        races(1, c, 0)
+
+    def meetings(c):
+        tx, rx, u, m = "tx%d" % c, "rx%d" % c, "u%d" % c, len(sides)
         both = lambda name, a, step: B(name, a + step * sides[0], a + step * sides[-1] + 1, step)
         at = lambda name, a=0, b=m, w=1: B(name, w * (4 * c + a), w * (4 * c + b))
-        if day:
-            tt(at("q1"), both(rx, 17, 2), both(tx, 1, 34), A.add)
-        else:
-            ts(at("ow"), both(tx, 1, 34), float(811 * 3), A.add)
-            tt(at("q1"), both(rx, 17, 2), at("ow"), A.add)
-            tt(at("q1", m, lb), both(rx, 17, 2), both("uw", 64 * c + 1, 253), A.add)
+        ts(at("ow"), both(tx, 1, 34), float(811 * 3), A.add)
+        tt(at("q1"), both(rx, 17, 2), at("ow"), A.add)
+        tt(at("q1", m, 2 * m), both(rx, 17, 2), both("uw", 64 * c + 1, 253), A.add)
         for l, i in enumerate(sides):
-            o, r = B(tx, 2 + 16 * i, 18 + 16 * i), B(rx, 20 * i, 20 * i + 16)
+            o, r, e = B(tx, 2 + 16 * i, 18 + 16 * i), B(rx, 20 * i, 20 * i + 16), own("xb", c, 61 * i, 61 * i + 1)
             tt(at("mc", l, l + 1, 16), o if i else r, r if i else o, A.subtract)
-            if not day:
-                e = own("xb", c, 61 * i, 61 * i + 1)
-                tt(at("mc", m + l, m + l + 1, 16), e if i else r, r if i else e, A.subtract)
-        ts(at("q2", 0, lb), at("q1", 0, lb), 8191, AND)
-        cp(at("hv", 0, lb), at("q2", 0, lb))
-        tt(at("mcmp", 0, lb, 16), IND(EW, at("hv", 0, lb)), at("mc", 0, lb, 16), A.is_gt)
-
-        def rows():
-            mm(B(u, 16, 16 + 16 * m), B("blk", 0, 128), at("mcmp", 0, m, 16), True, True)
-            ts(at("mw", 0, m, 16), B(u, 16, 16 + 16 * m), 11.5, A.is_gt)
-            tt(at("mm", 0, m, 16), at("mw", 0, m, 16), at("mc", 0, m, 16), A.mult)
-            for l, i in enumerate(sides):
-                new = B("fin", 48 * i + 16 * c, 48 * i + 16 * c + 16) if day else own("xb", c, 63 * i - 1, 63 * i)
-                tt(new, B(tx, 2 + 16 * i, 18 + 16 * i), at("mm", l, l + 1, 16), A.subtract if i else A.add)
-        if day:
-            rows()
-            u = "w%d" % c
+            tt(at("mc", m + l, m + l + 1, 16), e if i else r, r if i else e, A.subtract)
+        ts(at("q2", 0, 2 * m), at("q1", 0, 2 * m), 8191, AND)
+        cp(at("hv", 0, 2 * m), at("q2", 0, 2 * m))
+        tt(at("mcmp", 0, 2 * m, 16), IND(EW, at("hv", 0, 2 * m)), at("mc", 0, 2 * m, 16), A.is_gt)
+        mm(B(u, 0, 2 * m), IDP, B("kz", 0, 2 * m), True, False)
         for s in range(16):
-            mm(B(u, 0, lb), B("sel", 128 * s, 128 * s + 128), B("mcmp", 64 * c + s, 64 * c + 16 * lb, 16), s == 0, s == 15)
-        ts(at("nw"), B(u, 0, m), 11.5 * C, A.is_gt)
-        if day:
-            cp(at("p1"), both(rx, 17, 1))
-            ts(at("p2"), at("p1"), 8191, AND)
-            ts(at("p3"), at("p1"), 57344, AND)
-            ts(at("p4"), at("p2"), -4096.0, A.add, float(INV), A.mult)
-            ts(at("p1"), at("p4"), 8191, AND)
-            tt(at("pn"), at("p1"), at("p3"), A.add)
-            y = both("yn", c, 189)
-            tt(at("nd"), at("pn"), y, A.subtract)
-            tt(at("nm"), at("nw"), at("nd"), A.mult)
-            tt(y, y, at("nm"), A.add)
-            return
-        z, y = both(zat(c)[0], zat(c)[1] + 1, 62), both("va", 64 * c, 63)
-        ts(at("zz"), z, 11.5 * C, A.add)
-        tt(at("dz"), B(u, m, lb), at("zz"), A.subtract)
-        tt(at("zm"), at("nw"), at("dz"), A.mult)
-        tt(z, z, at("zm"), A.add)
+            mm(B(u, 0, 2 * m), B("sel", 128 * s, 128 * s + 128), B("mcmp", 64 * c + s, 64 * c + 32 * m, 16), False, s == 15)
+        ts(at("nw"), B(u, 0, m), 0.0, A.is_gt)
+        ts(at("nn"), B(u, 0, m), 0.0, A.is_le)
+        tt(at("zz"), B(u, m, 2 * m), at("nw"), A.mult)
         tt(at("nd"), both(rx, 17, 1), both(tx, 0, 35), A.subtract)
-        tt(at("nm"), at("nw"), at("nd"), A.mult)
-        tt(y, y, at("nm"), A.add)
+        for l, i in enumerate(sides):
+            z, y = Zc(c, 1 + 62 * i, 2 + 62 * i), L("NB", c, 63 * i, 63 * i + 1)
+            ts(z, z, at("nn", l, l + 1), A.mult, at("zz", l, l + 1), A.subtract)
+            ts(y, at("nd", l, l + 1), at("nw", l, l + 1), A.mult, y, A.add)
         if down:
-            f = UT(64 * c + 63, 64 * c + 64)
+            f = L("UT", c, 63)
             tt(at("nd", 2, 3), B(rx, 19, 20), f, A.subtract)
             tt(at("nm", 2, 3), at("nw", m - 1, m), at("nd", 2, 3), A.mult)
             tt(f, f, at("nm", 2, 3), A.add)
-        rows()
+        mm(B(u, 16, 16 + 16 * m), B("blk", 0, 128), at("mcmp", 0, m, 16), True, True)
+        ts(at("mw", 0, m, 16), B(u, 16, 16 + 16 * m), 11.5, A.is_gt)
+        tt(at("mm", 0, m, 16), at("mw", 0, m, 16), at("mc", 0, m, 16), A.mult)
+        for l, i in enumerate(sides):
+            tt(own("xb", c, 63 * i - 1, 63 * i), B(tx, 2 + 16 * i, 18 + 16 * i), at("mm", l, l + 1, 16), A.subtract if i else A.add)
 
-    def last_meetings(p):
-        n, c = len(p), p[0]
-        tx, rx, m, l0 = "tx%d" % (3 + c), "rx%d" % (3 + c), n * len(sides), 4 * c
-        at = lambda name, a=0, b=m, w=1: B(name, w * (l0 + a), w * (l0 + b))
+    def last_message():
+        for c in range(3):
+            places(c, B("hu", c, 6, 3), B("sv", c, c + 1))
+        ts(B("tx3", 9, 105), IND(B("xb", 0, 3 * CW), B("hu", 0, 6)), -UP, A.add)
+        for i in sides:
+            cp(B("tx3", 111 * i, 111 * i + 3), ends("n2", i))
+            cp(B("tx3", 3 + 105 * i, 6 + 105 * i), ends("n3", i))
+        if up:
+            ts(B("tx3", 6, 9), ends("n2", 0), float(BETA), A.mult, float(811 * 7 - MID), A.add)
+        message(3)
+
+    def last_meetings():
+        m = 3 * len(sides)
+        mine, theirs = lambda i: B("tx3", 9 + 48 * i, 57 + 48 * i), lambda i: B("rx3", 66 * i, 66 * i + 48)
+        ys = [B("yn", 189 * i, 189 * i + 3) for i in sides]
         for l, i in enumerate(sides):
-            u, w = (B(rx, 19 * n, 20 * n), B(tx, 35 * n, 36 * n)) if i else (B(tx, n, 2 * n), B(rx, 17 * n, 18 * n))
-            o, r = B(tx, (2 + 16 * i) * n, (18 + 16 * i) * n), B(rx, 20 * i * n, (20 * i + 16) * n)
-            tt(at("q1", n * l, n * l + n), u, w, A.add)
-            tt(at("mc", n * l, n * l + n, 16), o if i else r, r if i else o, A.subtract)
-        ts(at("q2"), at("q1"), 8191, AND)
-        cp(at("hv"), at("q2"))
-        tt(at("mcmp", 0, m, 16), IND(EW, at("hv")), at("mc", 0, m, 16), A.is_gt)
-        mw = B("vb", 400, 400 + 16 * m)
-        mm(B("u%d" % c, 0, 16 * m), B("blk", 0, 128), at("mcmp", 0, m, 16), True, True)
-        ts(mw, B("u%d" % c, 0, 16 * m), 11.5, A.is_gt)
-        tt(at("mm", 0, m, 16), mw, at("mc", 0, m, 16), A.mult)
+            u, w = (B("rx3", 63, 66), B("tx3", 111, 114)) if i else (B("tx3", 6, 9), B("rx3", 54, 57))
+            tt(B("q1", 3 * l, 3 * l + 3), u, w, A.add)
+            tt(B("mc", 48 * l, 48 * l + 48), mine(i) if i else theirs(i), theirs(i) if i else mine(i), A.subtract)
+            tt(B("zz", 3 * l, 3 * l + 3), B("rx3", 51 + 9 * i, 54 + 9 * i), ys[l], A.subtract)
+        ts(B("q2", 0, m), B("q1", 0, m), 8191, AND)
+        cp(B("hv", 0, m), B("q2", 0, m))
+        tt(B("mcmp", 0, 16 * m), IND(EW, B("hv", 0, m)), B("mc", 0, 16 * m), A.is_gt)
+        for o, k, b in (("u0", IDN, "blp"), ("u1", IDP, "bln")):
+            mm(B(o, 0, 16 * m), k, B("kg", 0, 16 * m), True, False)
+            mm(B(o, 0, 16 * m), B(b, 0, 128), B("mcmp", 0, 16 * m), False, True)
         for l, i in enumerate(sides):
-            tt(B("fin", 48 * i + 16 * c, 48 * i + 16 * (c + n)), B(tx, (2 + 16 * i) * n, (18 + 16 * i) * n), at("mm", n * l, n * l + n, 16), A.subtract if i else A.add)
+            tt(B("vb", 400 + 48 * l, 448 + 48 * l), theirs(i), B("u0", 48 * l, 48 * l + 48), A.min)
+        tt(B("fa", 0, 16 * m), B("tx3", 9 + 48 * sides[0], 57 + 48 * sides[-1]), B("u1", 0, 16 * m), A.min)
+        tt(B("fin", 48 * sides[0], 48 * sides[-1] + 48), B("vb", 400, 400 + 16 * m), B("fa", 0, 16 * m), A.max)
         for s in range(16):
-            mm(B("w%d" % c, 0, m), B("sel", 128 * s, 128 * s + 128), B("mcmp", 16 * l0 + s, 16 * (l0 + m), 16), s == 0, s == 15)
-        ts(at("nw"), B("w%d" % c, 0, m), 11.5 * C, A.is_gt)
-        cp(at("p1"), B(rx, (17 + sides[0]) * n, (17 + sides[0]) * n + m))
-        ts(at("p2"), at("p1"), 8191, AND)
-        ts(at("p3"), at("p1"), 57344, AND)
-        ts(at("p4"), at("p2"), -4096.0, A.add, float(INV), A.mult)
-        ts(at("p1"), at("p4"), 8191, AND)
-        tt(at("pn"), at("p1"), at("p3"), A.add)
-        ys = [B("yn", 189 * i + c, 189 * i + c + n) for i in sides]
+            mm(B("w0", 0, m), B("sel", 128 * s, 128 * s + 128), B("mcmp", s, 16 * m, 16), s == 0, s == 15)
+        ts(B("nw", 0, m), B("w0", 0, m), 11.5 * C, A.is_gt)
+        ts(B("p4", 0, m), B("rx3", 54 + 3 * sides[0], 54 + 3 * sides[0] + m), -4096.0, A.add, float(INV), A.mult)
+        ts(B("p1", 0, m), B("p4", 0, m), 8191, AND)
+        tt(B("nd", 0, m), B("p1", 0, m), B("zz", 0, m), A.add)
+        tt(B("nm", 0, m), B("nw", 0, m), B("nd", 0, m), A.mult)
         for l, y in enumerate(ys):
-            tt(at("nd", n * l, n * l + n), at("pn", n * l, n * l + n), y, A.subtract)
-        tt(at("nm"), at("nw"), at("nd"), A.mult)
-        for l, y in enumerate(ys):
-            tt(y, y, at("nm", n * l, n * l + n), A.add)
+            tt(y, y, B("nm", 3 * l, 3 * l + 3), A.add)
 
-    n1, n2, n3, ni = (B(k, 0, 192) for k in ("n1", "n2", "n3", "ni"))
     for c in range(3):
-        cp(B("n1", 64 * c, 64 * c + 64), B("bt", c, 192, 3))
-    ts(n2, n1, 101.0, A.mult, 4096.0, A.add)
-    ts(n3, n1, 57344, AND)
-    ts(ni, n2, 8191, AND)
-    ts(UT(0, 192), n1, 37.0, A.mult, 4096.0, A.add)
-    tt(WF(0, 192), ni, n3, A.add)
-    cp(ACC(0, 192), WF(0, 192))
-    for p in PARTS:
-        columns(p, 0)
-        place_words(p)
-    for c in range(3):
-        if c == RELAY:
-            ts(own("xa", c, -1, 63), IND(B("xn", 0, 3072), B("rl", 64 * c, 64 * c + 64)), UP, A.add)
-        else:
-            act(own("xa", c, -1, 63), IND(B("xn", 0, 3072), B("rl", 64 * c, 64 * c + 64)), bias=UP)
-        cp(xo(c), own("xa", c, 0, XO))
+        lead[0] = LEAD[c]
+        z = B("bt", c, 192, 3)
+        ts(L("ACC", c), z, 101.0, A.mult, 4096.0, A.add)
+        ts(L("UT", c), z, 37.0, A.mult, 4096.0, A.add)
+        columns(c, 0)
+        ts(L("n2", c), z, 101.0, A.mult, 4096.0, A.add)
+        ts(L("n3", c), z, 57344, AND)
+        ts(L("ni", c), L("n2", c), 8191, AND)
+        tt(L("NB", c), POS, L("n3", c), A.add)
+        tt(L("NB", c), L("NB", c), L("ni", c), A.add)
+        gather("v" if c in RELAY else "s", own("xa", c, -1, 63), IND(B("xn", 0, 3072), L("rl", c)), UP)
+        dma("y", xo(c), own("xa", c, 0, XO), "x%d" % c, WRAP, [EW])
     for c in range(3):
         races(0, c, 0)
     later_intervals(0)
-
-    for p in PARTS:
-        a, b = span(p)
-        post(p, 2)
-        ts(B("su", a, b), B("so", a, b), 16.0, A.mult, B("sv", 0, 1), A.add)
-        ts(WF(a, b), B("ni", a, b), 65535, AND)
-        ts(UT(a, b), B("n2", a, b), float(BETA), A.mult, float(811 * 3 - MID), A.add)
-        place_words(p)
-        columns(p, 0)
-        for c in p:
-            send(0, (c,))
-            act(own("xb", c, -1, 63), IND(win("xa", c), B("su", 64 * c, 64 * c + 64)))
-            dma("y", xo(c), own("xb", c, 0, XO), "x%d" % c)
     for c in range(3):
-        races(1, c, 0)
-    for c in range(3):
-        meetings(0, c)
+        post(c, 2)
+        night(c)
+        meetings(c)
     later_intervals(1)
 
-    for p in PARTS:
-        a, b = span(p)
-        post(p, 2)
-        ts(B("n3", a, b), B("ni", a, b), 57344, AND)
-        ts(B("n1", a, b), B("n2", a, b), -4096.0, A.add, float(INV), A.mult)
-        ts(B("ca", a, b), B("n1", a, b), 8191, AND)
-        for c in p:
-            ts(B("su", c, 192, 3), B("so", 64 * c, 64 * c + 64), 16.0, A.mult, B("sv", c, c + 1), A.add)
-            tt(B("yn", c, 192, 3), B("ca", 64 * c, 64 * c + 64), B("n3", 64 * c, 64 * c + 64), A.add)
-    for p in ENDS:
-        send(1, p)
+    for c in range(3):
+        post(c, 2)
+        ts(L("n3", c), L("ni", c), 57344, AND)
+        ts(L("n1", c), L("n2", c), -4096.0, A.add, float(INV), A.mult)
+        ts(L("ca", c), L("n1", c), 8191, AND)
+        ts(B("su", c, 192, 3), L("so", c), 16.0, A.mult, B("sv", c, c + 1), A.add)
+        tt(B("yn", c, 192, 3), L("ca", c), L("n3", c), A.add)
+    last_message()
     first, end = (48 if up else 0), (3024 if down else 3072)
-    lead[0] = 0.0
     for i, (e, q, a, b) in enumerate(OUT):
-        dst, src = B("outb", 16 * a, 16 * b), IND(B("xb", 0, 3 * CW), B("su", a, b))
-        if e == "s":
-            act(dst, src, bias=-UP)
-        else:
-            ts(dst, src, -UP, A.add)
+        gather(e, B("outb", 16 * a, 16 * b), IND(B("xb", 0, 3 * CW), B("su", a, b)), -UP)
         a, b = max(16 * a, first), min(16 * b, end)
         dma(q, T.yx[:, a:b], B("outb", a, b), "o%d" % i, 768 * i)
-    for p in ENDS:
-        last_meetings(p)
+    last_meetings()
     n = len(OUT)
     if up:
         dma("s", T.yx[:, 0:48], B("fin", 0, 48), "o%d" % n)

from concourse.bass import DstId, RemoteDMATransfer
from concourse.mybir import AluOpType, ActivationFunctionType

A = AluOpType
ACT = ActivationFunctionType
AND = A.bitwise_and
C = float(2 ** 25)
HUGE = float(2 ** 60)
ONE = 131072.0
MORE = 16000000
BIG = 1024.0
UP = 128.0
CW = 1040
WRAP = 1632
NV = (((40, 32, 20), (26, 26, 26), (26, 26, 26)), ((36, 24, 14), (26, 26, 26), (30, 30, 30)))
XO = max(_n for _d in NV for _k in _d[1:] for _n in _k)
NA = 50
PIECE = 16
RELAY = (1,)
SELG = 8
OUT = (("v", "y", 0, 48), ("s", "s", 96, 144), ("v", "y", 48, 96), ("s", "s", 144, 192))
CYCLE, GATHER, WAKE, CROSS, DMA0, RATE, WAY, FIRST = 0.00088, 1.56, 0.25, 0.23, 1.8, 550e3, 3.8, 1.5
AHEAD = 0.05
LEADS = ((2.0, 1.0, 0.0), (2.5, 1.5, 0.0), (3.0, 1.5, 0.0), (1.5, 1.0, 0.0))
LEAD = (0, 1, 2)
PASSES = 3


def centred(v):
    v %= 8192
    return v - 8192 if v >= 4096 else v


INV = centred(pow(101, -1, 8192))
BETA = centred(37 * INV)
MID = 8192 * 600

F, H, I, U = "float32", "bfloat16", "int32", "uint16"
SCRATCH = {}
for _n, _w, _t in (("xn", 3072, H), ("outb", 3072, H), ("ew", 8192 + WRAP, H), ("bt", 192, I), ("xa", 3 * CW, H), ("xb", 3 * CW, H), ("xo", 48 * XO, H),
                   ("sel", 2048, H), ("jb0", 128, H), ("jb1", 128, H), ("jb", 128, H), ("one", 128, H), ("idp", 128, H), ("idn", 128, H),
                   ("blk", 128, H), ("blc", 128, H), ("blp", 128, H), ("bln", 128, H), ("k0", 126, H), ("k1", 126, H), ("kg", 96, H), ("kz", 4, H), ("neg", 64, H),
                   ("pi", 1, I), ("pj", 1, I), ("pf", 1, F), ("sv", 3, F), ("ioc", 3, I), ("iol", 192, I), ("iob", 64, I), ("rl", 192, U),
                   ("n1", 192, I), ("n2", 192, I), ("n3", 192, I), ("uw", 384, I), ("ni", 192, I), ("so", 192, I), ("su", 192, U), ("yn", 192, F),
                   ("s0", 195, F), ("x0", 195, F), ("s", 192, F), ("vt", 192, F), ("xk", 192, F), ("t", 192, F), ("nk", 192, F), ("ys", 192, F),
                   ("ma", 192, H), ("mb", 192, H), ("cs", 192, I), ("ca", 192, I), ("oi", 192, I), ("cu", 192, U), ("of", 192, U),
                   ("hu", 6, U), ("hv", 12, U), ("q1", 12, I), ("q2", 12, I), ("mc", 192, F), ("mm", 192, F), ("mcmp", 192, H), ("mw", 192, F),
                   ("nd", 12, F), ("nw", 12, F), ("nn", 12, F), ("nm", 12, F), ("zz", 12, F), ("ow", 12, F), ("p1", 6, I), ("p4", 6, I),
                   ("fa", 96, F), ("fin", 96, H)):
    SCRATCH[_n] = ("sbuf", [128, _w], _t)
for _c in range(3):
    for _n in ("dv", "cmp", "xr", "es"):
        SCRATCH["%s_%d" % (_n, _c)] = ("sbuf", [128, 1008], H)
for _c in range(4):
    SCRATCH["tx%d" % _c] = SCRATCH["rx%d" % _c] = ("sbuf", [128, 36 if _c < 3 else 114], F)
PSUM = ("va", "vb", "u0", "u1", "u2", "w0", "w1", "w2")
Z = 448
for _n in PSUM:
    SCRATCH[_n] = ("psum", [128, 512], F)
QSEM = {"v": "qv", "s": "qs", "p": "qp", "g": "qg"}
SEMAPHORES = (["qv", "qs", "qp", "qg", "db", "dx", "de", "dw", "loc"] + ["x%d" % _c for _c in range(6)] + ["o%d" % _c for _c in range(len(OUT) + 3)]
              + ["r%s%d" % (_n, _c) for _n in "hf" for _c in range(4)])


def B(name, a, b, step=1):
    return (name, a, b, step)


def IND(w, o):
    return ("ind", w, o)


def entries(v):
    return entries(v[1]) + entries(v[2]) if v[0] == "ind" else [v]


def size(v):
    return 16 * size(v[2]) if v[0] == "ind" else len(range(v[1], v[2], abs(v[3])))


def meet(v, w):
    if v[0] != w[0] or v[1] >= w[2] or w[1] >= v[2]:
        return False
    return abs(v[3]) == abs(w[3]) == 1 or not set(range(v[1], v[2], abs(v[3]))).isdisjoint(range(w[1], w[2], abs(w[3])))


def own(x, c, j0, j1, shift=0):
    a = c * CW + 16 * (j0 + 2 + shift)
    return B(x, a, a + 16 * (j1 - j0))


def win(x, c):
    return B(x, c * CW, (c + 1) * CW)


def xo(c, j0=0, j1=XO):
    return B("xo", 16 * (c * XO + j0), 16 * (c * XO + j1))


LISTS = {"Y": ("va", 0, 64), "ACC": ("va", 192, 64), "R": ("vb", 0, 64), "NB": ("vb", 192, 65), "UT": ("uw", 0, 64), "WF": ("uw", 192, 64),
         "s0": ("s0", 0, 65), "x0": ("x0", 0, 65)}


def L(name, c, a=0, b=64, step=1):
    buf, first, stride = LISTS.get(name, (name, 0, 64))
    return B(buf, first + stride * c + a, first + stride * c + b, step)


def ends(name, i):
    buf, first, stride = LISTS.get(name, (name, 0, 64))
    return B(buf, first + 63 * i, first + 3 * stride, stride)


def M(k):
    return "mb" if k % 2 else "ma"


def t_(n, c, a, b, step=1):
    return B("%s_%d" % (n, c), a, b, step)


def Zc(c, a=1, b=64, step=1):
    return B("w%d" % c, Z + a, Z + b, step)


POS = B("va", 384, 448)
EW, EWX = B("ew", 0, 8192), B("ew", 0, 8192 + WRAP)
IDP, IDN, SV0 = B("idp", 0, 128), B("idn", 0, 128), B("sv", 0, 1)


def in_order(calls):
    seen = {}
    for i, c in enumerate(calls):
        c["after"] = set(c["after"])
        for kind, views in (("r", c["reads"]), ("w", c["writes"])):
            for v in views:
                for k2, w, j in seen.get(v[0], []):
                    bank = v[0] in PSUM and (calls[j]["q"] != c["q"] or c["q"] == "p")
                    if j != i and (bank or (meet(v, w) and "w" in (kind, k2))):
                        c["after"].add(j)
                old = seen.setdefault(v[0], [])
                if kind == "w" and v[3] == 1 and v[0] not in PSUM:
                    old[:] = [e for e in old if not (v[1] <= e[1][1] and e[1][2] <= v[2])]
                old.append((kind, v, i))
    gap = lambda j, i: CROSS if calls[j]["q"] != calls[i]["q"] else 0.0 if calls[i]["q"] == "p" else WAKE
    for c in calls:
        c["way"], c["next"] = c["time"], []
    for i in reversed(range(len(calls))):
        for j in calls[i]["after"]:
            calls[j]["way"] = max(calls[j]["way"], calls[j]["time"] + gap(j, i) + calls[i]["way"])
            calls[j]["next"].append(i)

    def longest_first(lead):
        free, order, end = {}, [], {}
        left = [len(c["after"]) for c in calls]
        ready = {i: 0.0 for i in range(len(calls)) if not left[i]}
        while ready:
            start = {i: max(t, free.get(calls[i]["q"], 0.0)) for i, t in ready.items()}
            first = min(start, key=lambda i: (start[i], i))
            q = calls[first]["q"]
            i = max((i for i in start if calls[i]["q"] == q and start[i] <= start[first] + AHEAD),
                    key=lambda i: (calls[i]["way"] + lead[calls[i]["chunk"]] - start[i], -i))
            del ready[i]
            free[q], end[i] = start[i] + calls[i]["hold"], start[i] + calls[i]["time"]
            order.append(i)
            for j in calls[i]["next"]:
                left[j] -= 1
                if not left[j]:
                    ready[j] = max(end[k] + gap(k, j) for k in calls[j]["after"])
        return order

    def place(order, behind):
        t, busy = {}, {}
        for i in order:
            a, n, line = max([t[j] + d for j, d in behind[i]] + [0.0]), calls[i]["hold"], busy.setdefault(calls[i]["q"], [])
            k = len(line)
            while k and line[k - 1][1] > a:
                k -= 1
            while k < len(line) and line[k][0] < a + n - 1e-9:
                a = max(a, line[k][1])
                k += 1
            line.insert(k, (a, a + n))
            t[i] = a
        return t
    forth = [[(j, calls[j]["time"] + gap(j, i)) for j in c["after"]] for i, c in enumerate(calls)]
    back = [[(j, calls[j]["hold"] + gap(i, j) + c["time"] - c["hold"]) for j in c["next"]] for i, c in enumerate(calls)]
    best = (1e9, None)
    for lead in LEADS:
        order = longest_first(lead)
        for _ in range(PASSES):
            t = place(order[::-1], back)
            order = sorted(order, key=lambda i: -t[i] - calls[i]["hold"])
            t = place(order, forth)
            order = sorted(order, key=lambda i: t[i])
            best = min(best, (max(t[i] + calls[i]["time"] for i in order), order))
    return best[1]


def rank_program(g, core, T, topo):
    rank = T.rank_of(core)
    if rank is None:
        return
    n_ranks = len(T.cores)
    up, down = rank > 0, rank < n_ranks - 1
    sides = [i for i, ok in ((0, up), (1, down)) if ok]
    queue = {"v": g.vector, "s": g.scalar, "p": g.tensor, "g": g, "y": g.sync}
    calls, lead = [], [2]

    def ap(v):
        if not isinstance(v, tuple):
            return v
        if v[0] == "ind":
            return ap(v[1]).indirect(ap(v[2]))
        name, a, b, step = v
        if step == -1:
            return T[name][:, b - 1:(a - 1 if a > 0 else None):-1]
        return T[name][:, a:b] if step == 1 else T[name][:, a:b:step]

    def note(q, reads, writes, call, time, hold=None, sem=None, n=1, after=()):
        flat = lambda views: [e for v in views if isinstance(v, tuple) for e in entries(v)]
        calls.append({"q": q, "reads": flat(reads), "writes": flat(writes), "call": call, "time": time, "hold": time if hold is None else hold,
                      "chunk": lead[0], "sem": sem or QSEM[q], "n": n, "after": after})
        return len(calls) - 1

    def op(q, reads, writes, call, cycles=None):
        n = size(writes[0])
        if reads and reads[0][0] == "ind":
            time = 0.06 + n * GATHER * CYCLE
        elif q == "p":
            time = max(64, n) * CYCLE / 2
        elif q == "g":
            time = 0.17 + 2 * n * CYCLE
        else:
            narrow = q == "v" and all(SCRATCH[v[0]][2] in (H, U) for v in reads[:2] + writes if isinstance(v, tuple))
            time = max(64, n * (cycles or (0.5 if narrow else 1))) * CYCLE
        note(q, reads, writes, call, time)

    def tt(out, a, b, o):
        op("v", [a, b], [out], lambda: g.vector.tensor_tensor(ap(out), ap(a), ap(b), o), 1 if a[0] in PSUM or b[0] in PSUM else 2)

    def ts(out, a, s1, o1, s2=None, o2=None):
        if o2 is None:
            op("v", [a, s1], [out], lambda: g.vector.tensor_scalar(ap(out), ap(a), ap(s1), None, o1))
        else:
            op("v", [a, s1, s2], [out], lambda: g.vector.tensor_scalar(ap(out), ap(a), ap(s1), ap(s2), o1, o2))

    def cp(out, a):
        op("v", [a], [out], lambda: g.vector.tensor_copy(ap(out), ap(a)))

    def scan(out, d0, d1, init, o0, o1):
        op("v", [d0, d1], [out], lambda: g.vector.tensor_tensor_scan(ap(out), ap(d0), ap(d1), init, o0, o1))

    def fill(out, val):
        op("v", [], [out], lambda: g.vector.memset(ap(out), val))

    def act(out, a, func=ACT.Copy, **kw):
        op("s", [a], [out], lambda: g.scalar.activation(ap(out), ap(a), func, **kw))

    def mm(out, lhs, rhs, start, stop):
        op("p", [lhs, rhs], [out], lambda: g.tensor.matmul(ap(out), ap(lhs), ap(rhs), start, stop))

    def dma(q, out, a, sem, before=0, behind=()):
        n = 256 * (before + size(out if isinstance(out, tuple) else a))
        note(q, [a, *behind], [out], lambda: queue[q].dma_start(ap(out), ap(a)), DMA0 + n / RATE, 0.05, sem, 16)

    def gi(out, pattern, base, cm):
        kw = {} if SCRATCH[out[0]][2] == I else {"allow_small_or_imprecise_dtypes": True}
        op("g", [], [out], lambda: g.iota(ap(out), pattern, base, cm, **kw))

    def gfill(out, val):
        gi(out, [[0, size(out)]], val, 0)

    def gsel(out, a, pattern, cmpop, val, base, cm):
        op("g", [a], [out], lambda: g.affine_select(ap(out), ap(a), pattern, cmpop, val, base, cm))

    def gather(e, out, src, add):
        if e == "s":
            act(out, src, bias=add)
        else:
            ts(out, src, add, A.add)

    dma("y", B("bt", 0, 192), T.boat[:], "db", 3072)
    dma("s", B("xn", 0, 3072), T.x[:], "dx")
    dma("y", EW, T.enc[:], "de", 3072)
    n_first = len(calls)
    dma("y", B("ew", 8192, 8192 + WRAP), T.enc[:, 0:WRAP], "dw", 0, [EW])

    gi(B("pi", 0, 1), [[0, 1]], 0, 1)
    gi(B("iol", 0, 192), [[16, 3], [48, 64]], 0, 0)
    gi(B("ioc", 0, 3), [[CW, 3]], 0, 0)
    gi(B("iob", 0, 64), [[1, 64]], 1, 0)
    gi(B("jb0", 0, 128), [[0, 8], [1, 16]], 0, 0)
    fill(B("one", 0, 128), 1.0)
    gsel(B("jb1", 0, 128), B("jb0", 0, 128), [[-16, 8], [0, 16]], A.is_ge, -1.0, 0, 1)
    gsel(B("jb", 0, 128), B("jb1", 0, 128), [[16, 8], [0, 16]], A.is_ge, -1.0, 15, -1)
    gsel(IDP, B("one", 0, 128), [[-1, 128]], A.is_equal, 0.0, 0, 1)
    ts(IDN, IDP, -1.0, A.mult)
    ts(B("pj", 0, 1), B("pi", 0, 1), 15, AND)
    cp(B("pf", 0, 1), B("pj", 0, 1))
    ts(B("rl", 0, 192), B("iol", 0, 192), B("pf", 0, 1), A.add)
    ts(B("sv", 0, 3), B("ioc", 0, 3), B("pf", 0, 1), A.add)
    ts(POS, B("iob", 0, 64), ONE, A.mult)
    fill(B("neg", 0, 64), -1.0)
    fill(ends("R", 0), 0.0)
    fill(B("vb", 256, 387, 65), 0.0)
    gfill(B("s0", 0, 195), MORE)
    gfill(B("x0", 0, 195), 0)
    gfill(B("s", 0, 192), -1)
    for x in ("xa", "xb"):
        for c in range(3):
            gfill(B(x, c * CW, c * CW + 16), 512)
    for k, v, s in (("k0", -4.5, 7.0), ("k1", -11.5, -7.0)):
        fill(B(k, 0, 63), v * C)
        fill(B(k, 63, 126), s * C)
    ts(B("blc", 0, 128), B("jb", 0, 128), 0.0, A.is_ge, C, A.mult)
    for s in range(16):
        if s < SELG:
            gsel(B("sel", 128 * s, 128 * s + 128), B("blc", 0, 128), [[0, 8], [1, 16]], A.is_equal, 0.0, -s, 0)
        else:
            ts(B("sel", 128 * s, 128 * s + 128), B("jb", 0, 128), float(s), A.is_equal, C, A.mult)
    for k, v in (("blk", 1.0), ("blp", BIG), ("bln", -BIG)):
        ts(B(k, 0, 128), B("jb", 0, 128), 0.0, A.is_ge, v, A.mult)
    gfill(B("kg", 0, 96), int(11.5 * BIG))
    fill(B("kz", 0, 4), -11.5 * C)
    for c in range(3):
        gfill(B("tx%d" % c, 34, 35), 0)
    gfill(B("tx3", 105, 108), 0)

    def columns(c, k):
        tt(L("cs", c, 0, 63), L("UT", c, 1), L("R", c, 1) if k else L("ACC", c, 0, 63), A.add)
        ts(L("ca", c, 0, 63), L("cs", c, 0, 63), 8191, AND)
        ts(L("cu", c, 0, 63), L("ca", c, 0, 63), float(811 * k), A.add)

    def races(day, c, k):
        x, nv, ew = "xb" if day else "xa", NV[day][k][c], EWX if k else EW
        lead[0] = LEAD[c]
        if not k:
            scan(t_("dv", c, 0, 16 * nv), own(x, c, 0, nv, -1), own(x, c, 0, nv), 0.0, A.max, A.subtract)
        for j0 in range(0, nv, PIECE):
            j1 = min(j0 + PIECE, nv)
            dv = t_("dv", c, 16 * j0, 16 * j1)
            if k:
                tt(dv, IND(win(x, c), L("of", c, j0, j1)), xo(c, j0, j1), A.subtract)
            tt(t_("cmp", c, 16 * j0, 16 * j1), IND(ew, L("cu", c, j0, j1)), dv, A.is_gt if k else A.is_le)
        na = min(nv + 32, NA)
        for u, j0, j1 in (("u", nv, na), ("w", na, 63)):
            o = B("%s%d" % (u, c), 0, 16 * (j1 - j0))
            xr, es = t_("xr", c, 16 * j0, 16 * j1), t_("es", c, 16 * j0, 16 * j1)
            mm(o, IDP, own(x, c, j0, j1), True, False)
            if k:
                act(xr, IND(win(x, c), L("of", c, j0, j1)))
            mm(o, IDN, xr if k else own(x, c, j0, j1, -1), False, False)
            act(es, IND(ew, L("cu", c, j0, j1)))
            mm(o, IDP, es, False, True)
            act(t_("cmp", c, 16 * j0, 16 * j1), o, ACT.Sign, bias=-0.5 if k else 0.5, scale=1.0 if k else -1.0)
        mm(Zc(c), IDP, B("k1" if k else "k0", 63 - nv, 126 - nv), True, False)
        if k:
            mm(Zc(c), IDP, L(M(k), c, 1), False, False)
        for s in range(16):
            mm(Zc(c), B("sel", 128 * s, 128 * s + 128), t_("cmp", c, s, 1008, 16), False, s == 15)

    def post(c, k):
        lead[0] = LEAD[c]
        Y, ACC, R, s, vt, t, x, nk, ys = (L(i, c) for i in ("Y", "ACC", "R", "s", "vt", "t", "xk", "nk", "ys"))
        neg, nbx = B("neg", 0, 63), L("NB", c, 1, 65)
        if not k:
            scan(L("s0", c, 1), neg, Zc(c), C, A.mult, A.max)
            tt(Y, L("NB", c), L("s0", c), A.min)
            tt(Y, Y, L("s0", c, 1, 65), A.min)
            ts(L("x0", c), L("s0", c), -1.0, A.mult, 0.0, A.max)
            tt(ACC, nbx, L("x0", c, 1, 65), A.min)
            tt(L("t", c, 1), L("NB", c, 0, 63), L("x0", c, 1), A.min)
            tt(L("ACC", c, 1), L("ACC", c, 1), L("t", c, 1), A.max)
        else:
            scan(L("s", c, 1), neg, Zc(c), -C, A.mult, A.min)
            tt(vt, Y, s, A.min)
            scan(L("NB", c, 0, 64, -1), L(M(k), c, 0, 64, -1), L("vt", c, 0, 64, -1), 0.0, A.min, A.max)
            ts(x, s, 0.0, A.max)
            tt(ys, Y, x, A.subtract)
            tt(nk, nbx, L(M(k), c), A.subtract)
        if k == 1:
            tt(Y, ys, nbx, A.subtract)
            tt(t, R, vt, A.min)
            tt(ACC, ACC, t, A.max)
            tt(ACC, ACC, nk, A.max)
        if k == 2:
            tt(ACC, ACC, ys, A.max)
            tt(ACC, ACC, nk, A.max)
            cp(L("ni", c), ACC)
            ts(L("so", c), ACC, 1 / ONE, A.mult, -0.25, A.add)
            ts(L("n2", c), L("ni", c), 8191, AND)
            return
        scan(L("R", c, 1), neg, L("Y", c, 0, 63), 0.0, A.max, A.max)
        ts(L(M(k + 1), c), Y, 0.0, A.is_le, HUGE, A.mult)
        ts(L("oi", c, 0, 63), L("R", c, 1), 1 / ONE, A.mult, -0.25, A.add)
        ts(L("of", c, 0, 63), L("oi", c, 0, 63), 16.0, A.mult, SV0, A.add)
        columns(c, k + 1)
        if k:
            tt(t, R, L(M(2), c), A.subtract)
            tt(ACC, ACC, t, A.max)

    def later_intervals(day):
        for k in range(2):
            for c in range(3):
                post(c, k)
                races(day, c, k + 1)

    def message(m):
        tx, rx = "tx%d" % m, "rx%d" % m
        w = SCRATCH[tx][1][1] // 2
        ways = ([(rank - 1, 0, w, "rh%d" % m)] if up else []) + ([(rank + 1, w, 0, "rf%d" % m)] if down else [])
        trs, n = [], 0
        for i, (r, a, b, sem) in enumerate(ways):
            es = topo.engines(core, T.cores[r])
            es = es[i * len(es) // len(ways):(i + 1) * len(es) // len(ways)]
            rid, pid, _ = topo.addr(T.cores[r])
            trs.append(RemoteDMATransfer(dst_ids=[DstId(rid=rid, pnc=pid)], dma_engine_mask=sum(1 << e for e in es), remote_sem=T.sem[sem],
                                         src=T[tx][:, a:a + w], dst=T[rx][:, b:b + w]))
            n += len(es)
        sent = note("g", [B(tx, 0, 2 * w)], [], lambda: g.remote_dma_fused(trs, local_sem=T.sem["loc"]), 0.3, None, "loc", n)
        for ok, r, a, sem in ((up, rank - 1, 0, "rf%d" % m), (down, rank + 1, w, "rh%d" % m)):
            if ok:
                fan = (1 if r > 0 else 0) + (1 if r < n_ranks - 1 else 0)
                note(sem, [], [B(rx, a, a + w)], None, WAY + (0 if m else FIRST), 0.0, sem, len(topo.engines(T.cores[r], core)) // fan, [sent])

    def places(c, out, base):
        ts(out, L("so", c, 0, 64, 63), 16.0, A.mult, base, A.add)

    def night(c):
        tx, hu = "tx%d" % c, B("hu", 2 * c, 2 * c + 2)
        ts(L("su", c), L("so", c), 16.0, A.mult, SV0, A.add)
        ts(L("WF", c), L("ni", c), 65535, AND)
        ts(L("UT", c), L("n2", c), float(BETA), A.mult, float(811 * 3 - MID), A.add)
        tt(L("NB", c), POS, L("WF", c), A.add)
        columns(c, 0)
        places(c, hu, SV0)
        cp(B(tx, 2, 34), IND(win("xa", c), hu))
        cp(B(tx, 0, 36, 35), L("WF", c, 0, 64, 63))
        ts(B(tx, 1, 2), L("n2", c, 0, 1), float(BETA), A.mult, float(811 * 3 - MID), A.add)
        message(c)
        for j in (0, 32):
            act(own("xb", c, j - 1, j + 31), IND(win("xa", c), L("su", c, j, j + 32)))
        dma("y", xo(c), own("xb", c, 0, XO), "x%d" % (3 + c))
        races(1, c, 0)

    def meetings(c):
        tx, rx, u, m = "tx%d" % c, "rx%d" % c, "u%d" % c, len(sides)
        both = lambda name, a, step: B(name, a + step * sides[0], a + step * sides[-1] + 1, step)
        at = lambda name, a=0, b=m, w=1: B(name, w * (4 * c + a), w * (4 * c + b))
        ts(at("ow"), both(tx, 1, 34), float(811 * 3), A.add)
        tt(at("q1"), both(rx, 17, 2), at("ow"), A.add)
        tt(at("q1", m, 2 * m), both(rx, 17, 2), both("uw", 64 * c + 1, 253), A.add)
        for l, i in enumerate(sides):
            o, r, e = B(tx, 2 + 16 * i, 18 + 16 * i), B(rx, 20 * i, 20 * i + 16), own("xb", c, 61 * i, 61 * i + 1)
            tt(at("mc", l, l + 1, 16), o if i else r, r if i else o, A.subtract)
            tt(at("mc", m + l, m + l + 1, 16), e if i else r, r if i else e, A.subtract)
        ts(at("q2", 0, 2 * m), at("q1", 0, 2 * m), 8191, AND)
        cp(at("hv", 0, 2 * m), at("q2", 0, 2 * m))
        tt(at("mcmp", 0, 2 * m, 16), IND(EW, at("hv", 0, 2 * m)), at("mc", 0, 2 * m, 16), A.is_gt)
        mm(B(u, 0, 2 * m), IDP, B("kz", 0, 2 * m), True, False)
        for s in range(16):
            mm(B(u, 0, 2 * m), B("sel", 128 * s, 128 * s + 128), B("mcmp", 64 * c + s, 64 * c + 32 * m, 16), False, s == 15)
        ts(at("nw"), B(u, 0, m), 0.0, A.is_gt)
        ts(at("nn"), B(u, 0, m), 0.0, A.is_le)
        tt(at("zz"), B(u, m, 2 * m), at("nw"), A.mult)
        tt(at("nd"), both(rx, 17, 1), both(tx, 0, 35), A.subtract)
        for l, i in enumerate(sides):
            z, y = Zc(c, 1 + 62 * i, 2 + 62 * i), L("NB", c, 63 * i, 63 * i + 1)
            ts(z, z, at("nn", l, l + 1), A.mult, at("zz", l, l + 1), A.subtract)
            ts(y, at("nd", l, l + 1), at("nw", l, l + 1), A.mult, y, A.add)
        if down:
            f = L("UT", c, 63)
            tt(at("nd", 2, 3), B(rx, 19, 20), f, A.subtract)
            tt(at("nm", 2, 3), at("nw", m - 1, m), at("nd", 2, 3), A.mult)
            tt(f, f, at("nm", 2, 3), A.add)
        mm(B(u, 16, 16 + 16 * m), B("blk", 0, 128), at("mcmp", 0, m, 16), True, True)
        ts(at("mw", 0, m, 16), B(u, 16, 16 + 16 * m), 11.5, A.is_gt)
        tt(at("mm", 0, m, 16), at("mw", 0, m, 16), at("mc", 0, m, 16), A.mult)
        for l, i in enumerate(sides):
            tt(own("xb", c, 63 * i - 1, 63 * i), B(tx, 2 + 16 * i, 18 + 16 * i), at("mm", l, l + 1, 16), A.subtract if i else A.add)

    def last_message():
        for c in range(3):
            places(c, B("hu", c, 6, 3), B("sv", c, c + 1))
        ts(B("tx3", 9, 105), IND(B("xb", 0, 3 * CW), B("hu", 0, 6)), -UP, A.add)
        for i in sides:
            cp(B("tx3", 111 * i, 111 * i + 3), ends("n2", i))
            cp(B("tx3", 3 + 105 * i, 6 + 105 * i), ends("n3", i))
        if up:
            ts(B("tx3", 6, 9), ends("n2", 0), float(BETA), A.mult, float(811 * 7 - MID), A.add)
        message(3)

    def last_meetings():
        m = 3 * len(sides)
        mine, theirs = lambda i: B("tx3", 9 + 48 * i, 57 + 48 * i), lambda i: B("rx3", 66 * i, 66 * i + 48)
        ys = [B("yn", 189 * i, 189 * i + 3) for i in sides]
        for l, i in enumerate(sides):
            u, w = (B("rx3", 63, 66), B("tx3", 111, 114)) if i else (B("tx3", 6, 9), B("rx3", 54, 57))
            tt(B("q1", 3 * l, 3 * l + 3), u, w, A.add)
            tt(B("mc", 48 * l, 48 * l + 48), mine(i) if i else theirs(i), theirs(i) if i else mine(i), A.subtract)
            tt(B("zz", 3 * l, 3 * l + 3), B("rx3", 51 + 9 * i, 54 + 9 * i), ys[l], A.subtract)
        ts(B("q2", 0, m), B("q1", 0, m), 8191, AND)
        cp(B("hv", 0, m), B("q2", 0, m))
        tt(B("mcmp", 0, 16 * m), IND(EW, B("hv", 0, m)), B("mc", 0, 16 * m), A.is_gt)
        for o, k, b in (("u0", IDN, "blp"), ("u1", IDP, "bln")):
            mm(B(o, 0, 16 * m), k, B("kg", 0, 16 * m), True, False)
            mm(B(o, 0, 16 * m), B(b, 0, 128), B("mcmp", 0, 16 * m), False, True)
        for l, i in enumerate(sides):
            tt(B("vb", 400 + 48 * l, 448 + 48 * l), theirs(i), B("u0", 48 * l, 48 * l + 48), A.min)
        tt(B("fa", 0, 16 * m), B("tx3", 9 + 48 * sides[0], 57 + 48 * sides[-1]), B("u1", 0, 16 * m), A.min)
        tt(B("fin", 48 * sides[0], 48 * sides[-1] + 48), B("vb", 400, 400 + 16 * m), B("fa", 0, 16 * m), A.max)
        for s in range(16):
            mm(B("w0", 0, m), B("sel", 128 * s, 128 * s + 128), B("mcmp", s, 16 * m, 16), s == 0, s == 15)
        ts(B("nw", 0, m), B("w0", 0, m), 11.5 * C, A.is_gt)
        ts(B("p4", 0, m), B("rx3", 54 + 3 * sides[0], 54 + 3 * sides[0] + m), -4096.0, A.add, float(INV), A.mult)
        ts(B("p1", 0, m), B("p4", 0, m), 8191, AND)
        tt(B("nd", 0, m), B("p1", 0, m), B("zz", 0, m), A.add)
        tt(B("nm", 0, m), B("nw", 0, m), B("nd", 0, m), A.mult)
        for l, y in enumerate(ys):
            tt(y, y, B("nm", 3 * l, 3 * l + 3), A.add)

    for c in range(3):
        lead[0] = LEAD[c]
        z = B("bt", c, 192, 3)
        ts(L("ACC", c), z, 101.0, A.mult, 4096.0, A.add)
        ts(L("UT", c), z, 37.0, A.mult, 4096.0, A.add)
        columns(c, 0)
        ts(L("n2", c), z, 101.0, A.mult, 4096.0, A.add)
        ts(L("n3", c), z, 57344, AND)
        ts(L("ni", c), L("n2", c), 8191, AND)
        tt(L("NB", c), POS, L("n3", c), A.add)
        tt(L("NB", c), L("NB", c), L("ni", c), A.add)
        gather("v" if c in RELAY else "s", own("xa", c, -1, 63), IND(B("xn", 0, 3072), L("rl", c)), UP)
        dma("y", xo(c), own("xa", c, 0, XO), "x%d" % c, WRAP, [EW])
    for c in range(3):
        races(0, c, 0)
    later_intervals(0)
    for c in range(3):
        post(c, 2)
        night(c)
        meetings(c)
    later_intervals(1)

    for c in range(3):
        post(c, 2)
        ts(L("n3", c), L("ni", c), 57344, AND)
        ts(L("n1", c), L("n2", c), -4096.0, A.add, float(INV), A.mult)
        ts(L("ca", c), L("n1", c), 8191, AND)
        ts(B("su", c, 192, 3), L("so", c), 16.0, A.mult, B("sv", c, c + 1), A.add)
        tt(B("yn", c, 192, 3), L("ca", c), L("n3", c), A.add)
    last_message()
    first, end = (48 if up else 0), (3024 if down else 3072)
    for i, (e, q, a, b) in enumerate(OUT):
        gather(e, B("outb", 16 * a, 16 * b), IND(B("xb", 0, 3 * CW), B("su", a, b)), -UP)
        a, b = max(16 * a, first), min(16 * b, end)
        dma(q, T.yx[:, a:b], B("outb", a, b), "o%d" % i, 768 * i)
    last_meetings()
    n = len(OUT)
    if up:
        dma("s", T.yx[:, 0:48], B("fin", 0, 48), "o%d" % n)
    if down:
        dma("y", T.yx[:, 3024:3072], B("fin", 48, 96), "o%d" % (n + 1))
    dma("y" if up else "s", T.yb[:], B("yn", 0, 192), "o%d" % (n + 2))

    count, waited = {}, {}

    def need(q, sem, val):
        if waited.get((q, sem), 0) < val:
            waited[(q, sem)] = val
            queue[q].wait_ge(T.sem[sem], val)
    order = in_order(calls)
    for i in list(range(n_first)) + [i for i in order if i >= n_first]:
        c = calls[i]
        count[c["sem"]] = c["val"] = count.get(c["sem"], 0) + c["n"]
        if c["call"]:
            waits = {}
            for j in c["after"]:
                if not calls[j]["q"] == c["q"] == "p":
                    waits[calls[j]["sem"]] = max(waits.get(calls[j]["sem"], 0), calls[j]["val"])
            for sem in sorted(waits):
                need(c["q"], sem, waits[sem])
            done = c["call"]()
            if c["sem"] != "loc":
                done.then_inc(T.sem[c["sem"]], c["n"])
    for sem in sorted(count):
        need("g", sem, count[sem])
